import numpy as np
import ml_dtypes


def mxq(x, axis, fmt="e4m3"):
    dtype, down = {"e4m3": (ml_dtypes.float8_e4m3fn, 7), "e5m2": (ml_dtypes.float8_e5m2, 14)}[fmt]
    v = np.moveaxis(np.asarray(x, np.float32).astype(ml_dtypes.bfloat16).astype(np.float64), axis, -1)
    blocks = v.reshape(v.shape[:-1] + (-1, 32))
    amax = np.abs(blocks).max(-1, keepdims=True)
    byte = np.maximum(np.where(amax > 0, np.frexp(amax)[1] - 1 + 127, 0) - down, 1)
    scale = np.exp2(byte - 127.0)
    codes = (blocks / scale).astype(np.float32).astype(dtype).astype(np.float64)
    return np.moveaxis((codes * scale).reshape(v.shape), -1, axis)


WIDE = False


def mx_kscale(k):
    if not WIDE:
        return np.ones(k)
    levels = np.array([10, -10, 5, -5, 0])
    if k % 512:
        return np.exp2(np.random.permutation(np.resize(levels, k // 32))).repeat(32)
    a = np.empty((k // 512, 16))
    for p in range(k // 512):
        a[p, :8] = np.random.permutation(np.resize(levels, 8))
        for g in range(8):
            far = levels[np.abs(levels - a[p, g]) >= 10]
            a[p, g + 8] = far[np.random.randint(len(far))]
    return np.exp2(a.ravel()).repeat(32)


BF16 = ml_dtypes.bfloat16


def bf(x):
    return np.asarray(x, np.float32).astype(BF16)


def f64(x):
    return np.asarray(x).astype(np.float64)


E2M1 = np.array([0.0, 0.5, 1.0, 1.5, 2.0, 3.0, 4.0, 6.0, -0.0, -0.5, -1.0, -1.5, -2.0, -3.0, -4.0, -6.0])


def pack_weight(w, fmt):
    k, n = w.shape
    w = f64(bf(w)).reshape(k // 32, 32, n)
    amax = np.abs(w).max(1)
    if fmt == "e4m3":
        byte = np.frexp(amax)[1] - 1 + 127 - 7
    else:
        mant, ex = np.frexp(amax / 6.0)
        byte = np.where(mant > 0.5, ex, ex - 1) + 127
    byte = np.clip(np.where(amax > 0, byte, 1), 1, 254)
    scaled = (w * np.exp2(127.0 - byte)[:, None, :]).reshape(k, n).astype(np.float32)
    by_word = np.ascontiguousarray(scaled.reshape(k // 512, 128, 4, n).transpose(0, 1, 3, 2))
    if fmt == "e4m3":
        words = by_word.astype(ml_dtypes.float8_e4m3fn).view(np.uint8)
    else:
        c = by_word.astype(ml_dtypes.float4_e2m1fn).view(np.uint8) & 0xF
        words = c[..., 0::2] | (c[..., 1::2] << 4)
    return np.ascontiguousarray(words), np.ascontiguousarray(byte.astype(np.uint8).reshape(k // 512, 16, n))


def unpack_weight(words, scales, fmt):
    g, p, n, _ = words.shape
    if fmt == "e4m3":
        vals = np.ascontiguousarray(words).view(ml_dtypes.float8_e4m3fn).astype(np.float64)
    else:
        nib = np.empty((g, p, n, 4), np.uint8)
        nib[..., 0::2] = words & 0xF
        nib[..., 1::2] = words >> 4
        vals = E2M1[nib]
    vals = vals * np.repeat(np.exp2(scales.astype(np.float64) - 127.0), 8, axis=1)[..., None]
    return vals.transpose(0, 1, 3, 2).reshape(g * 512, n)

E4M3FN = np.array([(-1.0 if i & 128 else 1.0) * ((1.0 + (i & 7) / 8.0) * 2.0 ** (((i >> 3) & 15) - 7) if i & 120 else (i & 7) * 2.0 ** -9) for i in range(256)])


def e4m3fn_bytes(y):
    return np.clip(np.asarray(y, np.float64), -448.0, 448.0).astype(np.float32).astype(ml_dtypes.float8_e4m3fn).view(np.uint8)


def e4m3fn_values(b):
    return E4M3FN[b]


B, E, D, F, O = 256, 8, 512, 1024, 512


def relu_relaxation(centre, generators):
    rad = np.sum(np.abs(generators), axis=1)
    l = centre - rad
    u = centre + rad
    lam = np.minimum(1.0, np.maximum(u, 0.0) / (2.0 * rad + 1e-6))
    mu = 0.5 * lam * np.maximum(-l, 0.0)
    return lam, mu


def draw0():
    s, t = mx_kscale(D), mx_kscale(F)
    c = np.random.standard_normal((B, D)) * 2.0
    gens = np.random.standard_normal((B, E, D)) * (3.2 / E)
    w1 = np.random.standard_normal((D, F)) / np.sqrt(D)
    b1 = np.random.standard_normal(F) * 0.5
    k = 1.0 + 0.1 * np.random.standard_normal(F)
    w2 = 1.5 * np.random.standard_normal((F, O)) / np.sqrt(F)
    w1_words, w1_scales = pack_weight(w1 / s[:, None], "e4m3")
    w2_words, w2_scales = pack_weight(w2 / t[:, None], "e4m3")
    return {"c": bf(c * s), "gens": bf(gens * s), "w1_words": w1_words, "w1_scales": w1_scales, "b1": bf(b1),
            "k": bf(k * t), "w2_words": w2_words, "w2_scales": w2_scales}


def core(c, gens, w1_words, w1_scales, b1, k, w2_words, w2_scales):
    w1q = unpack_weight(w1_words, w1_scales, "e4m3")
    c1 = (mxq(f64(c), 1, "e4m3") @ w1q) + f64(b1)
    g1 = mxq(f64(gens), 2, "e4m3") @ w1q

    lam, mu = relu_relaxation(c1, g1)

    kk = f64(k)
    w2q = unpack_weight(w2_words, w2_scales, "e4m3")
    hc = kk * (lam * c1 + mu)
    hg = kk * lam[:, None, :] * g1
    c2 = mxq(hc, 1, "e4m3") @ w2q
    g2 = mxq(hg, 2, "e4m3") @ w2q
    return g2, c2, mu


def setup_inputs():
    drawn = draw0()
    full = np.asarray(drawn['gens']).astype(np.float64)
    scale = (np.abs(full).reshape(256, 8, 4, 128).max(axis=(3,)) / 448.0).astype(np.float32)
    given = {}
    for key, value in drawn.items():
        if key == 'gens':
            given['gens_bytes'] = e4m3fn_bytes(full / np.repeat(scale.astype(np.float64), 128, axis=2))
            given['gens_scale'] = scale
        else:
            given[key] = value
    return given


def reference(c, gens_bytes, gens_scale, w1_words, w1_scales, b1, k, w2_words, w2_scales):
    return core(c, e4m3fn_values(gens_bytes) * np.repeat(gens_scale.astype(np.float64), 128, axis=2), w1_words, w1_scales, b1, k, w2_words, w2_scales)

@@ -1,0 +1,468 @@
+from contextlib import ExitStack
+
+import concourse.mybir as mybir
+from concourse.masks import make_identity
+
+F32 = mybir.dt.float32
+BF16 = mybir.dt.bfloat16
+I32 = mybir.dt.int32
+U32 = mybir.dt.uint32
+U8 = mybir.dt.uint8
+FP8 = mybir.dt.float8_e4m3fn
+FP8X4 = mybir.dt.float8_e4m3fn_x4
+ALU = mybir.AluOpType
+ACT = mybir.ActivationFunctionType
+AX = mybir.AxisListType
+
+B, E, D, F, O = 256, 8, 512, 1024, 512
+P = 128
+UB = 32
+UT = UB * E
+NU = B // UB
+NF = F // P
+EPS = 1e-6
+FLOPS = 2 * (B + B * E) * (D * F + F * O)
+A_UNITS = (2, 3, 4, 5, 6, 7)
+V_WIDEN = (4, 6, 8, 8, 8, 2, 6, 4)
+EXV = ()
+
+
+def tile_reluzonotopescaledgeneratormap_kernel(
+    tc, c, gens_bytes, gens_scale, w1_words, w1_scales, b1, k, w2_words, w2_scales, out_0, out_1, out_2
+):
+    nc = tc.nc
+    with ExitStack() as ctx:
+        keep = ctx.enter_context(tc.tile_pool(name="keep", bufs=1))
+        work = ctx.enter_context(tc.tile_pool(name="work", bufs=4))
+        outs = ctx.enter_context(tc.tile_pool(name="outs", bufs=4))
+        ps_x = ctx.enter_context(tc.psum_pool(name="ps_x", bufs=2))
+        ps_g = ctx.enter_context(tc.psum_pool(name="ps_g", bufs=2))
+        ps_r = ctx.enter_context(tc.psum_pool(name="ps_r", bufs=2))
+        ps_o = ctx.enter_context(tc.psum_pool(name="ps_o", bufs=2))
+
+        rows = gens_bytes.rearrange("b e d -> (b e) d")
+        raw = []
+
+        def load(u):
+            r = keep.tile([P, 2, D], U8, name="raw%d" % u, align_bytes=64)
+            nc.sync.dma_start(out=r[:], in_=rows[UT * u : UT * (u + 1), :].rearrange("(p j) d -> p j d", j=2))
+            raw.append(r)
+
+        w1s_raw = keep.tile([P, F], U8, name="w1s_raw", align_bytes=64)
+        w2s = keep.tile([P, 2, O], U8, name="w2s", align_bytes=64)
+        nc.vector.memset(w1s_raw[:].bitcast(I32), 0)
+        nc.vector.memset(w2s[:].rearrange("p g n -> p (g n)").bitcast(I32), 0)
+
+        load(0)
+        gsc = keep.tile([P, NU, 8], F32, name="gsc")
+        nc.sync.dma_start(out=gsc[:], in_=gens_scale.rearrange("b e q -> (b e q)").rearrange("(u p x) -> p u x", p=P, x=8))
+        load(1)
+        w1_raw = keep.tile([P, F], I32, name="w1_raw", align_bytes=64)
+        nc.sync.dma_start(out=w1_raw[:], in_=w1_words[0].rearrange("p n t -> p (n t)").bitcast(I32))
+        for q in range(4):
+            nc.scalar.dma_start(out=w1s_raw[32 * q : 32 * q + 4, :].bitcast(I32), in_=w1_scales[0, 4 * q : 4 * q + 4, :].bitcast(I32))
+        cb = keep.tile([P, 2, D], BF16, name="cb", align_bytes=64)
+        nc.sync.dma_start(out=cb[:], in_=c.rearrange("(p j) d -> p j d", j=2))
+        b1c = keep.tile([P, 2, 4], BF16, name="b1c")
+        nc.scalar.dma_start(out=b1c[:], in_=b1.rearrange("(g p t) -> p g t", g=2, t=4))
+        kc = keep.tile([P, 2, 4], BF16, name="kc")
+        nc.scalar.dma_start(out=kc[:], in_=k.rearrange("(g p t) -> p g t", g=2, t=4))
+        for u in range(2, 4):
+            load(u)
+        w2w = keep.tile([P, 2, O], I32, name="w2w", align_bytes=64)
+        nc.sync.dma_start(out=w2w[:], in_=w2_words.rearrange("g p n t -> p g (n t)").bitcast(I32))
+        for q in range(4):
+            nc.sync.dma_start(out=w2s[32 * q : 32 * q + 4, :, :].bitcast(I32), in_=w2_scales[:, 4 * q : 4 * q + 4, :].rearrange("g r n -> r g n").bitcast(I32))
+        for u in range(4, NU):
+            load(u)
+
+        ident = keep.tile([P, P], F32, name="ident")
+        make_identity(nc, ident[:])
+
+        w1p = keep.tile([P, F], I32, name="w1p", align_bytes=64)
+        w1sp = keep.tile([P, F], U8, name="w1sp", align_bytes=64)
+
+        def permute_w1():
+            nc.vector.tensor_copy(
+                out=w1p[:].rearrange("p (g t m) -> p g t m", g=2, t=4),
+                in_=w1_raw[:].rearrange("p (g m t) -> p g t m", g=2, t=4),
+            )
+            nc.vector.tensor_copy(
+                out=w1sp[:].rearrange("p (g t m) -> p g t m", g=2, t=4),
+                in_=w1s_raw[:].rearrange("p (g m t) -> p g t m", g=2, t=4),
+            )
+
+        c1b = keep.tile([P, NF, B], F32, name="c1b")
+        c1i = keep.tile([P, 2, B, 4], F32, name="c1i")
+        kful = keep.tile([P, 2, UB, 4], F32, name="kful")
+        mu_t = [keep.tile([P, NF, P], F32, name="mu%d" % h) for h in range(2)]
+        hc_t = [keep.tile([P, 2, P, 4], BF16, name="hc%d" % h, align_bytes=64) for h in range(2)]
+
+        st = {}
+
+        def widen(u):
+            xb = keep.tile([P, 2, D], BF16, name="xb", bufs=4, align_bytes=64)
+            for i in range(8):
+                j, q = divmod(i, 4)
+                src = raw[u][:, j, P * q : P * (q + 1)].bitcast(FP8)
+                dst = xb[:, j, P * q : P * (q + 1)]
+                if i < V_WIDEN[u]:
+                    nc.vector.tensor_scalar(out=dst, in0=src, scalar1=gsc[:, u, i : i + 1], scalar2=None, op0=ALU.mult)
+                else:
+                    nc.scalar.activation(out=dst, in_=src, func=ACT.Copy, scale=gsc[:, u, i : i + 1])
+            st["xb", u] = xb
+
+        def turn(u):
+            xb = cb if u == "c" else st["xb", u]
+            words = xb[:].rearrange("p j d -> p (j d)").bitcast(F32)
+            xt = ps_x.tile([P, 4, P], F32, name="tt")
+            for j in range(2):
+                for w in range(2):
+                    nc.tensor.transpose(xt[:, 2 * j + w, :], words[:, 256 * j + w : 256 * (j + 1) : 2], ident[:])
+            xg = keep.tile([P, UT, 4], BF16, name="xg", bufs=4, align_bytes=64)
+            nc.scalar.copy(
+                out=xg[:].rearrange("p n t -> p (n t)").bitcast(F32).rearrange("p (r a) -> p r a", a=4),
+                in_=xt[:].rearrange("p a r -> p r a"),
+            )
+            st["xg", u] = xg
+
+        def quant_x(u):
+            xq = keep.tile([P, UT], U32, name="xq%s" % u, align_bytes=64)
+            xs = keep.tile([P, UT], U8, name="xs%s" % u, align_bytes=64)
+            nc.vector.quantize_mx(out=xq[:].bitcast(FP8X4), scales=xs[:], in_=st["xg", u][:].rearrange("p n t -> p (n t)"))
+            st["xq", u] = (xq, xs)
+
+        def mx1(out, f, u, n0, n):
+            xq, xs = st["xq", u]
+            cols = slice(P * f, P * (f + 1))
+            nc.tensor.matmul_mx(
+                out=out,
+                lhsT=w1p[:, cols].bitcast(FP8X4),
+                lhsT_scale=w1sp[:, cols],
+                rhs=xq[:, n0 : n0 + n].bitcast(FP8X4),
+                rhs_scale=xs[:, n0 : n0 + n],
+                start=True,
+                stop=True,
+            )
+
+        def stage1(u, h):
+            bank = ps_g.tile([P, 2, UT], F32, name="gb")
+            for i in range(2):
+                mx1(bank[:, i, :], 2 * h + i, u, 0, UT)
+            if u == "c":
+                for i in range(2):
+                    f = 2 * h + i
+                    nc.scalar.activation(out=c1b[:, f, :], in_=bank[:, i, :], func=ACT.Identity, bias=b1c[:, f // 4, f % 4 : f % 4 + 1])
+            elif u in A_UNITS:
+                if h == 0:
+                    st["ab", u] = work.tile([P, 2, E, 4, UB], F32, name="ab", bufs=3, align_bytes=64)
+                nc.scalar.activation(
+                    out=st["ab", u][:, h // 2, :, 2 * (h % 2) : 2 * (h % 2) + 2, :],
+                    in_=bank[:].rearrange("p i (b e) -> p e i b", e=E),
+                    func=ACT.Abs,
+                )
+            else:
+                if h == 0:
+                    st["g1", u] = work.tile([P, NF, UB, E], F32, name="g1", bufs=2)
+                nc.scalar.copy(
+                    out=st["g1", u][:, 2 * h : 2 * h + 2, :, :].rearrange("p f b e -> p (f b e)"),
+                    in_=bank[:].rearrange("p i n -> p (i n)"),
+                )
+
+        def radius_sum(u):
+            rt = ps_x.tile([P, 2, P], F32, name="tt")
+            ab = st["ab", u]
+            for g in range(2):
+                for e in range(E):
+                    nc.tensor.matmul(
+                        out=rt[:, g, :],
+                        lhsT=ab[:, g, e, :, :].rearrange("p t b -> p (t b)"),
+                        rhs=ident[:],
+                        is_transpose=True,
+                        start=(e == 0),
+                        stop=(e == E - 1),
+                    )
+            rts = work.tile([P, 2, P], F32, name="rts", align_bytes=64)
+            nc.scalar.copy(out=rts[:], in_=rt[:])
+            st["rts", u] = rts
+
+        def radius_back(u):
+            rb = ps_x.tile([P, 2, P], F32, name="tt")
+            for g in range(2):
+                nc.tensor.transpose(rb[:, g, :], st["rts", u][:, g, :], ident[:])
+            st["rad", u] = rb[:].rearrange("p g (t b) -> p g b t", t=4)
+
+        def radius_reduce(u):
+            rad = work.tile([P, NF, UB], F32, name="rad")
+            nc.vector.tensor_reduce(
+                out=rad[:].rearrange("p f b -> p (f b)"),
+                in_=st["g1", u][:].rearrange("p f b e -> p (f b) e"),
+                axis=AX.X,
+                op=ALU.add,
+                apply_absolute_value=True,
+            )
+            st["rad", u] = rad[:].rearrange("p (g t) b -> p g b t", g=2)
+
+        def inverse(u):
+            rs = work.tile([P, 2, UB, 4], F32, name="rs")
+            nc.scalar.activation(out=rs[:], in_=st["rad", u], func=ACT.Abs_reciprocal_sqrt, scale=2.0, bias=EPS)
+            inv = work.tile([P, 2, UB, 4], F32, name="inv")
+            nc.scalar.activation(out=inv[:], in_=rs[:], func=ACT.Square)
+            st["inv", u] = inv
+
+        def pair_tiles(u):
+            if u % 2 == 0:
+                for n in ("l", "y", "klam"):
+                    st[n, u // 2] = work.tile([P, 2, 2 * UB, 4], F32, name=n)
+
+        def part(n, u):
+            return st[n, u // 2][:, :, UB * (u % 2) : UB * (u % 2 + 1), :]
+
+        def centre(b0, nb):
+            return c1i[:, :, b0 : b0 + nb, :]
+
+        def centre_layout(g):
+            nc.vector.tensor_copy(out=c1i[:, g, :, :], in_=c1b[:, 4 * g : 4 * g + 4, :].rearrange("p t b -> p b t"))
+
+        def spread_k():
+            nc.vector.tensor_copy(out=kful[:], in_=kc[:].unsqueeze(2).to_broadcast([P, 2, UB, 4]))
+
+        def slope(u):
+            pair_tiles(u)
+            x = work.tile([P, 2, UB, 4], F32, name="x")
+            nc.vector.scalar_tensor_tensor(out=x[:], in0=centre(UB * u, UB), scalar=0.5 * EPS, in1=st["inv", u][:], op0=ALU.subtract, op1=ALU.mult)
+            nc.scalar.activation(out=part("y", u), in_=x[:], func=ACT.Relu, bias=0.5)
+            nc.vector.tensor_tensor(out=part("l", u), in0=centre(UB * u, UB), in1=st["rad", u], op=ALU.subtract)
+
+        def slope2(u):
+            nc.vector.scalar_tensor_tensor(out=part("klam", u), in0=part("y", u), scalar=1.0, in1=kful[:], op0=ALU.min, op1=ALU.mult)
+
+        def centre_z(w):
+            z = work.tile([P, 2, 2 * UB, 4], F32, name="z")
+            nc.gpsimd.tensor_scalar(out=z[:], in0=st["l", w][:], scalar1=-0.5, scalar2=0.0, op0=ALU.mult, op1=ALU.max)
+            st["z", w] = z
+
+        def centre_mu(w):
+            h, v = divmod(w, 2)
+            nc.gpsimd.tensor_tensor(
+                out=mu_t[h][:, :, 2 * UB * v : 2 * UB * (v + 1)].rearrange("p (g t) b -> p g t b", g=2),
+                in0=st["z", w][:].rearrange("p g b t -> p g t b"),
+                in1=st["y", w][:].rearrange("p g b t -> p g t b"),
+                op=ALU.mult,
+            )
+
+        def centre_hc(w):
+            s = work.tile([P, 2, 2 * UB, 4], F32, name="s")
+            nc.gpsimd.tensor_tensor(out=s[:], in0=centre(2 * UB * w, 2 * UB), in1=st["z", w][:], op=ALU.add)
+            h, v = divmod(w, 2)
+            nc.gpsimd.tensor_tensor(out=hc_t[h][:, :, 2 * UB * v : 2 * UB * (v + 1), :], in0=st["klam", w][:], in1=s[:], op=ALU.mult)
+
+        def again(u, g, m):
+            gr = ps_r.tile([P, 4, P], F32, name="gr")
+            for t in range(4):
+                mx1(gr[:, t, :], 4 * g + t, u, P * m, P)
+            st["gr", u, g, m] = gr
+
+        def product(u, g, m):
+            if ("hb", u) not in st:
+                st["hb", u] = work.tile([P, 2, 2, P * 4], BF16, name="hb", align_bytes=64)
+            nb = UB // 2
+            fs = slice(4 * g, 4 * g + 4)
+            bs = slice(nb * m, nb * (m + 1))
+            if u in A_UNITS:
+                src = st["gr", u, g, m][:].rearrange("p t (b e) -> p b e t", e=E)
+            else:
+                src = st["g1", u][:, fs, bs, :].rearrange("p t b e -> p b e t")
+            nc.vector.tensor_tensor(
+                out=st["hb", u][:, m, g, :].rearrange("p (b e t) -> p b e t", e=E, t=4),
+                in0=src,
+                in1=part("klam", u)[:, g, bs, :].unsqueeze(2).to_broadcast([P, nb, E, 4]),
+                op=ALU.mult,
+            )
+
+        def quant_h(u, m, w):
+            if ("hq", u) not in st:
+                hq = work.tile([P, 2, 2, P], U32, name="hq", align_bytes=64)
+                hs = work.tile([P, 2, 2, P], U8, name="hs", align_bytes=64)
+                st["hq", u] = (hq, hs)
+            hq, hs = st["hq", u]
+            nc.vector.quantize_mx(
+                out=hq[:, m : m + w, :, :].rearrange("p m g n -> p (m g n)").bitcast(FP8X4),
+                scales=hs[:, m : m + w, :, :].rearrange("p m g n -> p (m g n)"),
+                in_=st["hb", u][:, m : m + w, :, :].rearrange("p m g n -> p (m g n)"),
+            )
+
+        def stage2(codes, scales, dst, on_vector=False):
+            ob = ps_o.tile([P, O], F32, name="ob")
+            for g in range(2):
+                nc.tensor.matmul_mx(
+                    out=ob[:],
+                    lhsT=codes[:, g, :].bitcast(FP8X4),
+                    lhsT_scale=scales[:, g, :],
+                    rhs=w2w[:, g, :].bitcast(FP8X4),
+                    rhs_scale=w2s[:, g, :],
+                    start=(g == 0),
+                    stop=(g == 1),
+                )
+            res = outs.tile([P, O], F32, name="res")
+            if on_vector:
+                nc.vector.tensor_copy(out=res[:], in_=ob[:])
+            else:
+                nc.scalar.copy(out=res[:], in_=ob[:])
+            nc.sync.dma_start(out=dst, in_=res[:])
+
+        g2 = out_0.rearrange("b e o -> (b e) o")
+
+        def finish(u, m):
+            hq, hs = st["hq", u]
+            r0 = UT * u + P * m
+            stage2(hq[:, m, :, :], hs[:, m, :, :], g2[r0 : r0 + P, :], on_vector=((u, m) in EXV))
+
+        def half_mu(h, g):
+            if g == 0:
+                st["ms", h] = outs.tile([P, 2, P, 4], F32, name="ms")
+            ms = st["ms", h]
+            om = ps_o.tile([P, 4, P], F32, name="ob")
+            for t in range(4):
+                nc.tensor.transpose(om[:, t, :], mu_t[h][:, 4 * g + t, :], ident[:])
+            nc.scalar.copy(out=ms[:, g, :, :], in_=om[:].rearrange("b t p -> b p t"))
+            if g == 1:
+                nc.sync.dma_start(out=out_2[P * h : P * (h + 1), :], in_=ms[:].rearrange("b g p t -> b (g p t)"))
+
+        def half_c2(h):
+            cq = work.tile([P, 2, P], U32, name="cq", align_bytes=64)
+            cs = work.tile([P, 2, P], U8, name="cs", align_bytes=64)
+            nc.vector.quantize_mx(
+                out=cq[:].rearrange("p g n -> p (g n)").bitcast(FP8X4),
+                scales=cs[:].rearrange("p g n -> p (g n)"),
+                in_=hc_t[h][:].rearrange("p g n t -> p (g n t)"),
+            )
+            st["cq", h] = (cq, cs)
+
+        def half_c2_out(h):
+            stage2(st["cq", h][0], st["cq", h][1], out_1[P * h : P * (h + 1), :])
+
+        def radius_start(u):
+            if u in A_UNITS:
+                radius_sum(u)
+            else:
+                radius_reduce(u)
+                inverse(u)
+
+        def radius_end(u):
+            if u in A_UNITS:
+                radius_back(u)
+                inverse(u)
+
+        def recompute(u, g, m):
+            if u in A_UNITS:
+                again(u, g, m)
+
+        ctx.enter_context(tc.manual_schedule())
+        widen(0)
+        widen(1)
+        permute_w1()
+        turn(0)
+        quant_x(0)
+        radius_end(0)
+        recompute(0, 0, 0)
+        widen(3)
+        widen(2)
+        turn(1)
+        radius_end(1)
+        quant_x(1)
+        turn("c")
+        stage1(0, 0)
+        stage1(0, 3)
+        stage1(0, 1)
+        turn(2)
+        stage1(1, 0)
+        widen(4)
+        stage1(0, 2)
+        stage1(1, 3)
+        stage1(1, 1)
+        stage1(1, 2)
+        quant_x("c")
+        stage1("c", 1)
+        spread_k()
+        stage1("c", 2)
+        stage1("c", 3)
+        recompute(0, 1, 0)
+        quant_x(2)
+        stage1(2, 0)
+        stage1("c", 0)
+        radius_start(0)
+        stage1(2, 3)
+        turn(3)
+        turn(4)
+        centre_layout(1)
+        radius_start(1)
+        centre_layout(0)
+        quant_x(3)
+        slope(0)
+        stage1(2, 2)
+        stage1(2, 1)
+        slope2(0)
+        for u in range(NU + 1):
+            if u < NU:
+                recompute(u, 1, 1)
+            if u < NU and u % 2 == 1:
+                centre_hc(u // 2)
+            if u + 3 < NU:
+                stage1(u + 3, 0)
+            if u < NU:
+                product(u, 0, 0)
+            if u < NU and u % 2 == 1:
+                centre_mu(u // 2)
+            if u + 1 < NU:
+                slope(u + 1)
+            if u + 5 < NU:
+                widen(u + 5)
+            if u > 0:
+                finish(u - 1, 0)
+            if u % 4 == 3:
+                half_c2(u // 4)
+            if u < NU:
+                recompute(u, 0, 1)
+            if u < NU:
+                product(u, 1, 1)
+            if u + 3 < NU:
+                stage1(u + 3, 3)
+            if u % 4 == 3:
+                half_c2_out(u // 4)
+            if u + 2 < NU:
+                radius_start(u + 2)
+            if u % 4 == 3:
+                half_mu(u // 4, 0)
+            if u + 5 < NU:
+                turn(u + 5)
+            if u < NU:
+                product(u, 1, 0)
+            if u + 1 < NU:
+                recompute(u + 1, 1, 0)
+            if u == NU - 1:
+                quant_h(u, 0, 1)
+            if u < NU:
+                product(u, 0, 1)
+            if u + 1 < NU:
+                slope2(u + 1)
+            if u + 3 < NU:
+                stage1(u + 3, 2)
+            if u == NU - 1:
+                quant_h(u, 1, 1)
+            if u + 4 < NU:
+                quant_x(u + 4)
+            if u + 1 < NU:
+                recompute(u + 1, 0, 0)
+            if u + 1 < NU and u % 2 == 0:
+                centre_z((u + 1) // 2)
+            if u + 2 < NU:
+                radius_end(u + 2)
+            if u % 4 == 3:
+                half_mu(u // 4, 1)
+            if u > 0:
+                finish(u - 1, 1)
+            if u < NU - 1:
+                quant_h(u, 0, 2)
+            if u + 3 < NU:
+                stage1(u + 3, 1)

@@ -23,8 +23,8 @@ NF = F // P
 EPS = 1e-6
 FLOPS = 2 * (B + B * E) * (D * F + F * O)
 A_UNITS = (2, 3, 4, 5, 6, 7)
-V_WIDEN = (4, 6, 8, 8, 8, 2, 6, 4)
-EXV = ()
+V_WIDEN = (4, 6, 8, 8, 4, 4, 0, 4)
+EXV = ((7, 1), (7, 0))
 
 
 def tile_reluzonotopescaledgeneratormap_kernel(
@@ -169,22 +169,22 @@ def tile_reluzonotopescaledgeneratormap_kernel(
                     in_=bank[:].rearrange("p i n -> p (i n)"),
                 )
 
-        def radius_sum(u):
-            rt = ps_x.tile([P, 2, P], F32, name="tt")
-            ab = st["ab", u]
-            for g in range(2):
-                for e in range(E):
-                    nc.tensor.matmul(
-                        out=rt[:, g, :],
-                        lhsT=ab[:, g, e, :, :].rearrange("p t b -> p (t b)"),
-                        rhs=ident[:],
-                        is_transpose=True,
-                        start=(e == 0),
-                        stop=(e == E - 1),
-                    )
-            rts = work.tile([P, 2, P], F32, name="rts", align_bytes=64)
-            nc.scalar.copy(out=rts[:], in_=rt[:])
-            st["rts", u] = rts
+        def radius_sum(u, g):
+            if g == 0:
+                st["rt", u] = ps_x.tile([P, 2, P], F32, name="tt")
+            rt = st["rt", u]
+            for e in range(E):
+                nc.tensor.matmul(
+                    out=rt[:, g, :],
+                    lhsT=st["ab", u][:, g, e, :, :].rearrange("p t b -> p (t b)"),
+                    rhs=ident[:],
+                    is_transpose=True,
+                    start=(e == 0),
+                    stop=(e == E - 1),
+                )
+            if g == 1:
+                st["rts", u] = work.tile([P, 2, P], F32, name="rts", align_bytes=64)
+                nc.scalar.copy(out=st["rts", u][:], in_=rt[:])
 
         def radius_back(u):
             rb = ps_x.tile([P, 2, P], F32, name="tt")
@@ -239,12 +239,12 @@ def tile_reluzonotopescaledgeneratormap_kernel(
 
         def centre_z(w):
             z = work.tile([P, 2, 2 * UB, 4], F32, name="z")
-            nc.gpsimd.tensor_scalar(out=z[:], in0=st["l", w][:], scalar1=-0.5, scalar2=0.0, op0=ALU.mult, op1=ALU.max)
+            nc.scalar.activation(out=z[:], in_=st["l", w][:], func=ACT.Relu, scale=-0.5)
             st["z", w] = z
 
         def centre_mu(w):
             h, v = divmod(w, 2)
-            nc.gpsimd.tensor_tensor(
+            nc.vector.tensor_tensor(
                 out=mu_t[h][:, :, 2 * UB * v : 2 * UB * (v + 1)].rearrange("p (g t) b -> p g t b", g=2),
                 in0=st["z", w][:].rearrange("p g b t -> p g t b"),
                 in1=st["y", w][:].rearrange("p g b t -> p g t b"),
@@ -253,9 +253,9 @@ def tile_reluzonotopescaledgeneratormap_kernel(
 
         def centre_hc(w):
             s = work.tile([P, 2, 2 * UB, 4], F32, name="s")
-            nc.gpsimd.tensor_tensor(out=s[:], in0=centre(2 * UB * w, 2 * UB), in1=st["z", w][:], op=ALU.add)
+            nc.vector.tensor_tensor(out=s[:], in0=centre(2 * UB * w, 2 * UB), in1=st["z", w][:], op=ALU.add)
             h, v = divmod(w, 2)
-            nc.gpsimd.tensor_tensor(out=hc_t[h][:, :, 2 * UB * v : 2 * UB * (v + 1), :], in0=st["klam", w][:], in1=s[:], op=ALU.mult)
+            nc.vector.tensor_tensor(out=hc_t[h][:, :, 2 * UB * v : 2 * UB * (v + 1), :], in0=st["klam", w][:], in1=s[:], op=ALU.mult)
 
         def again(u, g, m):
             gr = ps_r.tile([P, 4, P], F32, name="gr")
@@ -342,10 +342,10 @@ def tile_reluzonotopescaledgeneratormap_kernel(
         def half_c2_out(h):
             stage2(st["cq", h][0], st["cq", h][1], out_1[P * h : P * (h + 1), :])
 
-        def radius_start(u):
+        def radius_start(u, g):
             if u in A_UNITS:
-                radius_sum(u)
-            else:
+                radius_sum(u, g)
+            elif g == 0:
                 radius_reduce(u)
                 inverse(u)
 
@@ -359,110 +359,114 @@ def tile_reluzonotopescaledgeneratormap_kernel(
                 again(u, g, m)
 
         ctx.enter_context(tc.manual_schedule())
-        widen(0)
+        recompute(0, 1, 0)
         widen(1)
+        widen(0)
+        turn(1)
         permute_w1()
         turn(0)
-        quant_x(0)
-        radius_end(0)
-        recompute(0, 0, 0)
-        widen(3)
-        widen(2)
-        turn(1)
-        radius_end(1)
-        quant_x(1)
         turn("c")
+        quant_x(0)
+        radius_end(1)
         stage1(0, 0)
-        stage1(0, 3)
-        stage1(0, 1)
-        turn(2)
-        stage1(1, 0)
-        widen(4)
+        quant_x(1)
         stage1(0, 2)
+        stage1(1, 0)
+        widen(3)
+        quant_x("c")
+        spread_k()
+        stage1(0, 3)
+        widen(2)
+        stage1(0, 1)
         stage1(1, 3)
+        radius_end(0)
+        stage1("c", 1)
+        stage1("c", 3)
+        recompute(0, 0, 0)
         stage1(1, 1)
         stage1(1, 2)
-        quant_x("c")
-        stage1("c", 1)
-        spread_k()
-        stage1("c", 2)
-        stage1("c", 3)
-        recompute(0, 1, 0)
-        quant_x(2)
-        stage1(2, 0)
         stage1("c", 0)
-        radius_start(0)
-        stage1(2, 3)
-        turn(3)
-        turn(4)
+        turn(2)
+        radius_start(0, 1)
+        radius_start(0, 0)
+        stage1("c", 2)
+        radius_start(1, 0)
+        quant_x(2)
         centre_layout(1)
-        radius_start(1)
+        turn(3)
+        widen(4)
+        stage1(2, 0)
         centre_layout(0)
-        quant_x(3)
+        radius_start(1, 1)
         slope(0)
-        stage1(2, 2)
         stage1(2, 1)
+        quant_x(3)
+        turn(4)
         slope2(0)
+        stage1(2, 3)
+        stage1(2, 2)
         for u in range(NU + 1):
-            if u < NU:
-                recompute(u, 1, 1)
+            if u > 0:
+                finish(u - 1, 0)
             if u < NU and u % 2 == 1:
-                centre_hc(u // 2)
+                centre_mu(u // 2)
+            if u < NU:
+                product(u, 1, 0)
+            if u + 5 < NU:
+                widen(u + 5)
             if u + 3 < NU:
                 stage1(u + 3, 0)
             if u < NU:
-                product(u, 0, 0)
-            if u < NU and u % 2 == 1:
-                centre_mu(u // 2)
-            if u + 1 < NU:
-                slope(u + 1)
-            if u + 5 < NU:
-                widen(u + 5)
-            if u > 0:
-                finish(u - 1, 0)
-            if u % 4 == 3:
-                half_c2(u // 4)
-            if u < NU:
                 recompute(u, 0, 1)
             if u < NU:
-                product(u, 1, 1)
-            if u + 3 < NU:
-                stage1(u + 3, 3)
-            if u % 4 == 3:
-                half_c2_out(u // 4)
-            if u + 2 < NU:
-                radius_start(u + 2)
+                product(u, 0, 0)
+            if u < NU and u % 2 == 1:
+                centre_hc(u // 2)
             if u % 4 == 3:
                 half_mu(u // 4, 0)
-            if u + 5 < NU:
-                turn(u + 5)
-            if u < NU:
-                product(u, 1, 0)
-            if u + 1 < NU:
-                recompute(u + 1, 1, 0)
-            if u == NU - 1:
-                quant_h(u, 0, 1)
-            if u < NU:
-                product(u, 0, 1)
-            if u + 1 < NU:
-                slope2(u + 1)
-            if u + 3 < NU:
-                stage1(u + 3, 2)
-            if u == NU - 1:
-                quant_h(u, 1, 1)
+            if u + 2 < NU:
+                radius_start(u + 2, 0)
             if u + 4 < NU:
                 quant_x(u + 4)
             if u + 1 < NU:
-                recompute(u + 1, 0, 0)
-            if u + 1 < NU and u % 2 == 0:
-                centre_z((u + 1) // 2)
-            if u + 2 < NU:
-                radius_end(u + 2)
+                slope(u + 1)
+            if u < NU:
+                recompute(u, 1, 1)
+            if u + 3 < NU:
+                stage1(u + 3, 2)
             if u % 4 == 3:
                 half_mu(u // 4, 1)
+            if u < NU:
+                product(u, 0, 1)
+            if u + 1 < NU and u % 2 == 0:
+                centre_z((u + 1) // 2)
+            if u % 4 == 3:
+                half_c2(u // 4)
+            if u + 2 < NU:
+                radius_start(u + 2, 1)
+            if u == NU - 1:
+                quant_h(u, 0, 1)
+            if u < NU:
+                product(u, 1, 1)
             if u > 0:
                 finish(u - 1, 1)
-            if u < NU - 1:
-                quant_h(u, 0, 2)
+            if u + 3 < NU:
+                stage1(u + 3, 3)
+            if u + 1 < NU:
+                recompute(u + 1, 1, 0)
             if u + 3 < NU:
                 stage1(u + 3, 1)
+            if u + 1 < NU:
+                recompute(u + 1, 0, 0)
+            if u + 5 < NU:
+                turn(u + 5)
+            if u + 1 < NU:
+                slope2(u + 1)
+            if u + 2 < NU:
+                radius_end(u + 2)
+            if u == NU - 1:
+                quant_h(u, 1, 1)
+            if u % 4 == 3:
+                half_c2_out(u // 4)
+            if u < NU - 1:
+                quant_h(u, 0, 2)

@@ -22,9 +22,9 @@ NU = B // UB
 NF = F // P
 EPS = 1e-6
 FLOPS = 2 * (B + B * E) * (D * F + F * O)
-A_UNITS = (2, 3, 4, 5, 6, 7)
-V_WIDEN = (4, 6, 8, 8, 4, 4, 0, 4)
-EXV = ((7, 1), (7, 0))
+A_UNITS = (1, 2, 3, 4, 5, 6, 7)
+V_WIDEN = (4, 8, 4, 6, 6, 0, 2, 6)
+EXV = ()
 
 
 def tile_reluzonotopescaledgeneratormap_kernel(
@@ -53,9 +53,11 @@ def tile_reluzonotopescaledgeneratormap_kernel(
         nc.vector.memset(w1s_raw[:].bitcast(I32), 0)
         nc.vector.memset(w2s[:].rearrange("p g n -> p (g n)").bitcast(I32), 0)
 
-        load(0)
         gsc = keep.tile([P, NU, 8], F32, name="gsc")
-        nc.sync.dma_start(out=gsc[:], in_=gens_scale.rearrange("b e q -> (b e q)").rearrange("(u p x) -> p u x", p=P, x=8))
+        scales = gens_scale.rearrange("b e q -> (b e q)").rearrange("(u p x) -> p u x", p=P, x=8)
+        nc.sync.dma_start(out=gsc[:, 0:1, :], in_=scales[:, 0:1, :])
+        load(0)
+        nc.sync.dma_start(out=gsc[:, 1:NU, :], in_=scales[:, 1:NU, :])
         load(1)
         w1_raw = keep.tile([P, F], I32, name="w1_raw", align_bytes=64)
         nc.sync.dma_start(out=w1_raw[:], in_=w1_words[0].rearrange("p n t -> p (n t)").bitcast(I32))
@@ -92,7 +94,7 @@ def tile_reluzonotopescaledgeneratormap_kernel(
                 in_=w1s_raw[:].rearrange("p (g m t) -> p g t m", g=2, t=4),
             )
 
-        c1b = keep.tile([P, NF, B], F32, name="c1b")
+        b1f = keep.tile([P, 2, 4], F32, name="b1f")
         c1i = keep.tile([P, 2, B, 4], F32, name="c1i")
         kful = keep.tile([P, 2, UB, 4], F32, name="kful")
         mu_t = [keep.tile([P, NF, P], F32, name="mu%d" % h) for h in range(2)]
@@ -149,11 +151,7 @@ def tile_reluzonotopescaledgeneratormap_kernel(
             bank = ps_g.tile([P, 2, UT], F32, name="gb")
             for i in range(2):
                 mx1(bank[:, i, :], 2 * h + i, u, 0, UT)
-            if u == "c":
-                for i in range(2):
-                    f = 2 * h + i
-                    nc.scalar.activation(out=c1b[:, f, :], in_=bank[:, i, :], func=ACT.Identity, bias=b1c[:, f // 4, f % 4 : f % 4 + 1])
-            elif u in A_UNITS:
+            if u in A_UNITS:
                 if h == 0:
                     st["ab", u] = work.tile([P, 2, E, 4, UB], F32, name="ab", bufs=3, align_bytes=64)
                 nc.scalar.activation(
@@ -210,25 +208,30 @@ def tile_reluzonotopescaledgeneratormap_kernel(
             nc.scalar.activation(out=inv[:], in_=rs[:], func=ACT.Square)
             st["inv", u] = inv
 
-        def pair_tiles(u):
-            if u % 2 == 0:
-                for n in ("l", "y", "klam"):
-                    st[n, u // 2] = work.tile([P, 2, 2 * UB, 4], F32, name=n)
-
         def part(n, u):
+            if (n, u // 2) not in st:
+                st[n, u // 2] = work.tile([P, 2, 2 * UB, 4], F32, name=n)
             return st[n, u // 2][:, :, UB * (u % 2) : UB * (u % 2 + 1), :]
 
         def centre(b0, nb):
             return c1i[:, :, b0 : b0 + nb, :]
 
-        def centre_layout(g):
-            nc.vector.tensor_copy(out=c1i[:, g, :, :], in_=c1b[:, 4 * g : 4 * g + 4, :].rearrange("p t b -> p b t"))
+        def stage1_centre(h, g):
+            bank = ps_g.tile([P, 4, P], F32, name="gb")
+            for t in range(4):
+                mx1(bank[:, t, :], 4 * g + t, "c", P * h, P)
+            nc.vector.tensor_tensor(
+                out=c1i[:, g, P * h : P * (h + 1), :],
+                in0=bank[:].rearrange("p t b -> p b t"),
+                in1=b1f[:, g, :].unsqueeze(1).to_broadcast([P, P, 4]),
+                op=ALU.add,
+            )
 
         def spread_k():
+            nc.vector.tensor_copy(out=b1f[:], in_=b1c[:])
             nc.vector.tensor_copy(out=kful[:], in_=kc[:].unsqueeze(2).to_broadcast([P, 2, UB, 4]))
 
         def slope(u):
-            pair_tiles(u)
             x = work.tile([P, 2, UB, 4], F32, name="x")
             nc.vector.scalar_tensor_tensor(out=x[:], in0=centre(UB * u, UB), scalar=0.5 * EPS, in1=st["inv", u][:], op0=ALU.subtract, op1=ALU.mult)
             nc.scalar.activation(out=part("y", u), in_=x[:], func=ACT.Relu, bias=0.5)
@@ -359,114 +362,111 @@ def tile_reluzonotopescaledgeneratormap_kernel(
                 again(u, g, m)
 
         ctx.enter_context(tc.manual_schedule())
-        recompute(0, 1, 0)
-        widen(1)
         widen(0)
-        turn(1)
+        widen(1)
         permute_w1()
         turn(0)
-        turn("c")
-        quant_x(0)
-        radius_end(1)
-        stage1(0, 0)
+        turn(1)
         quant_x(1)
-        stage1(0, 2)
-        stage1(1, 0)
-        widen(3)
-        quant_x("c")
-        spread_k()
-        stage1(0, 3)
         widen(2)
-        stage1(0, 1)
-        stage1(1, 3)
+        quant_x(0)
         radius_end(0)
-        stage1("c", 1)
-        stage1("c", 3)
+        turn("c")
+        stage1(1, 0)
+        spread_k()
+        stage1(0, 0)
+        stage1(0, 2)
+        recompute(0, 1, 0)
+        radius_start(0, 1)
+        stage1(0, 3)
+        stage1(0, 1)
         recompute(0, 0, 0)
         stage1(1, 1)
         stage1(1, 2)
-        stage1("c", 0)
+        quant_x("c")
+        stage1(1, 3)
+        widen(3)
         turn(2)
-        radius_start(0, 1)
         radius_start(0, 0)
-        stage1("c", 2)
-        radius_start(1, 0)
-        quant_x(2)
-        centre_layout(1)
+        stage1_centre(0, 0)
+        stage1_centre(0, 1)
         turn(3)
-        widen(4)
-        stage1(2, 0)
-        centre_layout(0)
-        radius_start(1, 1)
         slope(0)
+        radius_start(1, 0)
+        radius_start(1, 1)
+        quant_x(2)
+        radius_end(1)
+        stage1(2, 0)
         stage1(2, 1)
-        quant_x(3)
-        turn(4)
         slope2(0)
-        stage1(2, 3)
         stage1(2, 2)
+        widen(4)
         for u in range(NU + 1):
-            if u > 0:
-                finish(u - 1, 0)
-            if u < NU and u % 2 == 1:
-                centre_mu(u // 2)
-            if u < NU:
-                product(u, 1, 0)
-            if u + 5 < NU:
-                widen(u + 5)
-            if u + 3 < NU:
-                stage1(u + 3, 0)
-            if u < NU:
-                recompute(u, 0, 1)
             if u < NU:
                 product(u, 0, 0)
             if u < NU and u % 2 == 1:
+                centre_mu(u // 2)
+            if u > 0:
+                finish(u - 1, 0)
+            if u < NU:
+                product(u, 1, 0)
+            if u < NU and u % 2 == 1:
                 centre_hc(u // 2)
+            if u < NU:
+                recompute(u, 0, 1)
+            if u + 2 < NU:
+                stage1(u + 2, 3)
+            if u + 1 < NU:
+                slope(u + 1)
+            if u + 3 < NU:
+                quant_x(u + 3)
+            if u < NU:
+                recompute(u, 1, 1)
+            if u + 1 < NU and u % 2 == 0:
+                centre_z((u + 1) // 2)
+            if u < NU:
+                product(u, 0, 1)
+            if u == 1:
+                stage1_centre(1, 1)
             if u % 4 == 3:
                 half_mu(u // 4, 0)
             if u + 2 < NU:
                 radius_start(u + 2, 0)
+            if u % 4 == 3:
+                half_c2(u // 4)
+            if u > 0:
+                finish(u - 1, 1)
+            if u == NU - 1:
+                quant_h(u, 0, 1)
             if u + 4 < NU:
-                quant_x(u + 4)
+                turn(u + 4)
+            if u == 1:
+                stage1_centre(1, 0)
+            if u % 4 == 3:
+                half_mu(u // 4, 1)
             if u + 1 < NU:
-                slope(u + 1)
+                recompute(u + 1, 0, 0)
+            if u + 3 < NU:
+                stage1(u + 3, 0)
+            if u + 2 < NU:
+                radius_start(u + 2, 1)
+            if u + 3 < NU:
+                stage1(u + 3, 1)
             if u < NU:
-                recompute(u, 1, 1)
+                product(u, 1, 1)
+            if u == NU - 1:
+                quant_h(u, 1, 1)
+            if u + 1 < NU:
+                recompute(u + 1, 1, 0)
+            if u + 2 < NU:
+                radius_end(u + 2)
             if u + 3 < NU:
                 stage1(u + 3, 2)
             if u % 4 == 3:
-                half_mu(u // 4, 1)
-            if u < NU:
-                product(u, 0, 1)
-            if u + 1 < NU and u % 2 == 0:
-                centre_z((u + 1) // 2)
-            if u % 4 == 3:
-                half_c2(u // 4)
-            if u + 2 < NU:
-                radius_start(u + 2, 1)
-            if u == NU - 1:
-                quant_h(u, 0, 1)
-            if u < NU:
-                product(u, 1, 1)
-            if u > 0:
-                finish(u - 1, 1)
-            if u + 3 < NU:
-                stage1(u + 3, 3)
-            if u + 1 < NU:
-                recompute(u + 1, 1, 0)
-            if u + 3 < NU:
-                stage1(u + 3, 1)
-            if u + 1 < NU:
-                recompute(u + 1, 0, 0)
+                half_c2_out(u // 4)
             if u + 5 < NU:
-                turn(u + 5)
+                widen(u + 5)
             if u + 1 < NU:
                 slope2(u + 1)
-            if u + 2 < NU:
-                radius_end(u + 2)
-            if u == NU - 1:
-                quant_h(u, 1, 1)
-            if u % 4 == 3:
-                half_c2_out(u // 4)
             if u < NU - 1:
                 quant_h(u, 0, 2)

@@ -16,15 +16,46 @@ AX = mybir.AxisListType
 
 B, E, D, F, O = 256, 8, 512, 1024, 512
 P = 128
+G = F // 512
 UB = 32
 UT = UB * E
 NU = B // UB
-NF = F // P
+HB = 128
+PAIR = 2 * UB
 EPS = 1e-6
 FLOPS = 2 * (B + B * E) * (D * F + F * O)
-A_UNITS = (1, 2, 3, 4, 5, 6, 7)
-V_WIDEN = (4, 8, 4, 6, 6, 0, 2, 6)
-EXV = ()
+
+CENTRE = "c"
+REDUCED = (0,)
+
+VECTOR_PIECES = (8, 0, 8, 8, 6, 0, 0, 6)
+
+PROLOGUE = (
+    ("widen", 1, 0), ("widen", 0, 0), ("widen", 1, 1), ("widen", 0, 1), ("permute_w1", 0), ("turn", 0),
+    ("turn_out", 0), ("turn", 1), ("quantise_x", 0), ("widen", 2, 0), ("turn_out", 1), ("widen", 2, 1),
+    ("turn", CENTRE), ("stage1", 0, 0), ("turn_out", CENTRE), ("stage1", 0, 1), ("stage1_out", 0, 0),
+    ("stage1", 0, 3), ("widen", 3, 0), ("quantise_x", 1), ("stage1_out", 0, 1), ("stage1", 1, 0),
+    ("stage1_out", 0, 3), ("stage1", 0, 2), ("stage1_out", 1, 0), ("stage1", 1, 1), ("stage1_out", 0, 2),
+    ("widen", 3, 1), ("quantise_x", CENTRE), ("stage1", 1, 2), ("stage1_out", 1, 1), ("stage1_out", 1, 2),
+    ("widen", 4, 0), ("spread_constants", 0), ("stage1", 1, 3), ("turn", 2), ("centre_stage1", 0, 0),
+    ("stage1_out", 1, 3), ("centre_stage1", 0, 1), ("turn_out", 2), ("widen", 4, 1), ("radius_sum", 1, 1),
+    ("turn", 3), ("radius_sum", 0, 0), ("centre_stage1_out", 0, 0), ("centre_stage1_out", 0, 1), ("inverse", 0),
+    ("quantise_x", 2), ("radius_sum", 1, 0), ("turn_out", 3), ("slope_x", 0), ("slope_y", 0), ("radius_out", 1),
+    ("stage1", 2, 0), ("stage1", 2, 1), ("stage1_out", 2, 0), ("stage1_out", 2, 1), ("radius_back", 1),
+    ("slope_l", 0), ("inverse", 1), ("slope_klam", 0),
+)
+LOOP = (
+    ("centre_mu", 0), ("product", 0, 0, 0), ("stage2", -1, 0), ("product", 0, 1, 0), ("mu_turn", 0, 0),
+    ("stage1", 2, 3), ("stage1_again", 0, 0, 1), ("stage1", 2, 2), ("stage2_out", -1, 0), ("stage1_again", 0, 1, 1),
+    ("radius_sum", 2, 0), ("quantise_x", 3), ("centre_h", 0), ("mu_out", 0, 0), ("slope_l", 1), ("slope_x", 1),
+    ("mu_turn", 0, 1), ("stage1_out", 2, 3), ("centre_stage1", 3, 0), ("stage2", -1, 1), ("stage1_out", 2, 2),
+    ("mu_out", 0, 1), ("centre_stage1", 3, 1), ("quantise_h_part", 0, 0), ("centre_quantise", 0), ("turn", 4),
+    ("product", 0, 0, 1), ("widen", 5, 0), ("centre_stage1_out", 3, 0), ("slope_y", 1), ("centre_stage1_out", 3, 1),
+    ("centre_z", 1), ("stage2_out", -1, 1), ("widen", 5, 1), ("radius_sum", 2, 1), ("stage1", 3, 0),
+    ("stage1_again", 1, 0, 0), ("turn_out", 4), ("radius_out", 2), ("stage1_out", 3, 0), ("stage1", 3, 1),
+    ("product", 0, 1, 1), ("stage1_again", 1, 1, 0), ("radius_back", 2), ("stage1_out", 3, 1), ("slope_klam", 1),
+    ("quantise_h_part", 0, 1), ("centre_stage2", 0), ("quantise_h", 0), ("inverse", 2), ("centre_stage2_out", 0),
+)
 
 
 def tile_reluzonotopescaledgeneratormap_kernel(
@@ -49,7 +80,7 @@ def tile_reluzonotopescaledgeneratormap_kernel(
             raw.append(r)
 
         w1s_raw = keep.tile([P, F], U8, name="w1s_raw", align_bytes=64)
-        w2s = keep.tile([P, 2, O], U8, name="w2s", align_bytes=64)
+        w2s = keep.tile([P, G, O], U8, name="w2s", align_bytes=64)
         nc.vector.memset(w1s_raw[:].bitcast(I32), 0)
         nc.vector.memset(w2s[:].rearrange("p g n -> p (g n)").bitcast(I32), 0)
 
@@ -62,411 +93,402 @@ def tile_reluzonotopescaledgeneratormap_kernel(
         w1_raw = keep.tile([P, F], I32, name="w1_raw", align_bytes=64)
         nc.sync.dma_start(out=w1_raw[:], in_=w1_words[0].rearrange("p n t -> p (n t)").bitcast(I32))
         for q in range(4):
-            nc.scalar.dma_start(out=w1s_raw[32 * q : 32 * q + 4, :].bitcast(I32), in_=w1_scales[0, 4 * q : 4 * q + 4, :].bitcast(I32))
-        cb = keep.tile([P, 2, D], BF16, name="cb", align_bytes=64)
-        nc.sync.dma_start(out=cb[:], in_=c.rearrange("(p j) d -> p j d", j=2))
-        b1c = keep.tile([P, 2, 4], BF16, name="b1c")
-        nc.scalar.dma_start(out=b1c[:], in_=b1.rearrange("(g p t) -> p g t", g=2, t=4))
-        kc = keep.tile([P, 2, 4], BF16, name="kc")
-        nc.scalar.dma_start(out=kc[:], in_=k.rearrange("(g p t) -> p g t", g=2, t=4))
+            nc.scalar.dma_start(
+                out=w1s_raw[32 * q : 32 * q + 4, :].bitcast(I32), in_=w1_scales[0, 4 * q : 4 * q + 4, :].bitcast(I32)
+            )
+        c_rows = keep.tile([P, 2, D], BF16, name="c_rows", align_bytes=64)
+        nc.sync.dma_start(out=c_rows[:], in_=c.rearrange("(p j) d -> p j d", j=2))
+        b1_raw = keep.tile([P, G, 4], BF16, name="b1_raw")
+        nc.scalar.dma_start(out=b1_raw[:], in_=b1.rearrange("(g p t) -> p g t", g=G, t=4))
+        k_raw = keep.tile([P, G, 4], BF16, name="k_raw")
+        nc.scalar.dma_start(out=k_raw[:], in_=k.rearrange("(g p t) -> p g t", g=G, t=4))
         for u in range(2, 4):
             load(u)
-        w2w = keep.tile([P, 2, O], I32, name="w2w", align_bytes=64)
+        w2w = keep.tile([P, G, O], I32, name="w2w", align_bytes=64)
         nc.sync.dma_start(out=w2w[:], in_=w2_words.rearrange("g p n t -> p g (n t)").bitcast(I32))
         for q in range(4):
-            nc.sync.dma_start(out=w2s[32 * q : 32 * q + 4, :, :].bitcast(I32), in_=w2_scales[:, 4 * q : 4 * q + 4, :].rearrange("g r n -> r g n").bitcast(I32))
+            nc.sync.dma_start(
+                out=w2s[32 * q : 32 * q + 4, :, :].bitcast(I32),
+                in_=w2_scales[:, 4 * q : 4 * q + 4, :].rearrange("g r n -> r g n").bitcast(I32),
+            )
         for u in range(4, NU):
             load(u)
 
         ident = keep.tile([P, P], F32, name="ident")
         make_identity(nc, ident[:])
 
-        w1p = keep.tile([P, F], I32, name="w1p", align_bytes=64)
-        w1sp = keep.tile([P, F], U8, name="w1sp", align_bytes=64)
+        w1w = keep.tile([P, F], I32, name="w1w", align_bytes=64)
+        w1s = keep.tile([P, F], U8, name="w1s", align_bytes=64)
+        b1_f32 = keep.tile([P, G, 4], F32, name="b1_f32")
+        k_spread = keep.tile([P, G, UB, 4], F32, name="k_spread")
+        c1 = keep.tile([P, G, B, 4], F32, name="c1")
+        mu = [keep.tile([P, 2 * 4, HB], F32, name="mu%d" % h) for h in range(2)]
+        hc = [keep.tile([P, G, HB, 4], BF16, name="hc%d" % h, align_bytes=64) for h in range(2)]
+        made = {}
 
-        def permute_w1():
+        def permute_w1(u):
             nc.vector.tensor_copy(
-                out=w1p[:].rearrange("p (g t m) -> p g t m", g=2, t=4),
-                in_=w1_raw[:].rearrange("p (g m t) -> p g t m", g=2, t=4),
+                out=w1w[:].rearrange("p (g t m) -> p g t m", g=G, t=4),
+                in_=w1_raw[:].rearrange("p (g m t) -> p g t m", g=G, t=4),
             )
             nc.vector.tensor_copy(
-                out=w1sp[:].rearrange("p (g t m) -> p g t m", g=2, t=4),
-                in_=w1s_raw[:].rearrange("p (g m t) -> p g t m", g=2, t=4),
+                out=w1s[:].rearrange("p (g t m) -> p g t m", g=G, t=4),
+                in_=w1s_raw[:].rearrange("p (g m t) -> p g t m", g=G, t=4),
             )
 
-        b1f = keep.tile([P, 2, 4], F32, name="b1f")
-        c1i = keep.tile([P, 2, B, 4], F32, name="c1i")
-        kful = keep.tile([P, 2, UB, 4], F32, name="kful")
-        mu_t = [keep.tile([P, NF, P], F32, name="mu%d" % h) for h in range(2)]
-        hc_t = [keep.tile([P, 2, P, 4], BF16, name="hc%d" % h, align_bytes=64) for h in range(2)]
+        def spread_constants(u):
+            nc.vector.tensor_copy(out=b1_f32[:], in_=b1_raw[:])
+            nc.vector.tensor_copy(out=k_spread[:], in_=k_raw[:].unsqueeze(2).to_broadcast([P, G, UB, 4]))
 
-        st = {}
-
-        def widen(u):
-            xb = keep.tile([P, 2, D], BF16, name="xb", bufs=4, align_bytes=64)
-            for i in range(8):
-                j, q = divmod(i, 4)
+        def widen(u, j):
+            if j == 0:
+                made["x", u] = keep.tile([P, 2, D], BF16, name="x_rows", bufs=4, align_bytes=64)
+            for q in range(4):
+                i = 4 * j + q
                 src = raw[u][:, j, P * q : P * (q + 1)].bitcast(FP8)
-                dst = xb[:, j, P * q : P * (q + 1)]
-                if i < V_WIDEN[u]:
-                    nc.vector.tensor_scalar(out=dst, in0=src, scalar1=gsc[:, u, i : i + 1], scalar2=None, op0=ALU.mult)
+                dst = made["x", u][:, j, P * q : P * (q + 1)]
+                if 4 * (q % 2) + 2 * j + q // 2 < VECTOR_PIECES[u]:
+                    nc.vector.tensor_scalar(
+                        out=dst, in0=src, scalar1=gsc[:, u, i : i + 1], scalar2=None, op0=ALU.mult
+                    )
                 else:
                     nc.scalar.activation(out=dst, in_=src, func=ACT.Copy, scale=gsc[:, u, i : i + 1])
-            st["xb", u] = xb
 
         def turn(u):
-            xb = cb if u == "c" else st["xb", u]
-            words = xb[:].rearrange("p j d -> p (j d)").bitcast(F32)
-            xt = ps_x.tile([P, 4, P], F32, name="tt")
+            x_rows = c_rows if u == CENTRE else made["x", u]
+            words = x_rows[:].rearrange("p j d -> p (j d)").bitcast(F32)
+            bank = ps_x.tile([P, 4, P], F32, name="turned")
             for j in range(2):
                 for w in range(2):
-                    nc.tensor.transpose(xt[:, 2 * j + w, :], words[:, 256 * j + w : 256 * (j + 1) : 2], ident[:])
-            xg = keep.tile([P, UT, 4], BF16, name="xg", bufs=4, align_bytes=64)
-            nc.scalar.copy(
-                out=xg[:].rearrange("p n t -> p (n t)").bitcast(F32).rearrange("p (r a) -> p r a", a=4),
-                in_=xt[:].rearrange("p a r -> p r a"),
-            )
-            st["xg", u] = xg
+                    nc.tensor.transpose(bank[:, 2 * j + w, :], words[:, 256 * j + w : 256 * (j + 1) : 2], ident[:])
+            made["turned", u] = bank
 
-        def quant_x(u):
+        def turn_out(u):
+            xk = keep.tile([P, UT, 4], BF16, name="xk", bufs=4, align_bytes=64)
+            nc.scalar.copy(
+                out=xk[:].rearrange("p n t -> p (n t)").bitcast(F32).rearrange("p (r a) -> p r a", a=4),
+                in_=made["turned", u][:].rearrange("p a r -> p r a"),
+            )
+            made["xk", u] = xk
+
+        def quantise_x(u):
             xq = keep.tile([P, UT], U32, name="xq%s" % u, align_bytes=64)
             xs = keep.tile([P, UT], U8, name="xs%s" % u, align_bytes=64)
-            nc.vector.quantize_mx(out=xq[:].bitcast(FP8X4), scales=xs[:], in_=st["xg", u][:].rearrange("p n t -> p (n t)"))
-            st["xq", u] = (xq, xs)
+            nc.vector.quantize_mx(
+                out=xq[:].bitcast(FP8X4), scales=xs[:], in_=made["xk", u][:].rearrange("p n t -> p (n t)")
+            )
+            made["xq", u] = (xq, xs)
 
-        def mx1(out, f, u, n0, n):
-            xq, xs = st["xq", u]
+        def matmul1(out, f, u, n0, n):
+            xq, xs = made["xq", u]
             cols = slice(P * f, P * (f + 1))
             nc.tensor.matmul_mx(
                 out=out,
-                lhsT=w1p[:, cols].bitcast(FP8X4),
-                lhsT_scale=w1sp[:, cols],
+                lhsT=w1w[:, cols].bitcast(FP8X4),
+                lhsT_scale=w1s[:, cols],
                 rhs=xq[:, n0 : n0 + n].bitcast(FP8X4),
                 rhs_scale=xs[:, n0 : n0 + n],
                 start=True,
                 stop=True,
             )
 
+        def centre_stage1(u, g):
+            if u % (NU // 2) == 0:
+                bank = ps_g.tile([P, 4, P], F32, name="bank1")
+                for t in range(4):
+                    matmul1(bank[:, t, :], 4 * g + t, CENTRE, UB * u, HB)
+                made["bank_c", u, g] = bank
+
+        def centre_stage1_out(u, g):
+            if u % (NU // 2) == 0:
+                nc.vector.tensor_tensor(
+                    out=c1[:, g, UB * u : UB * u + HB, :],
+                    in0=made["bank_c", u, g][:].rearrange("p t b -> p b t"),
+                    in1=b1_f32[:, g, :].unsqueeze(1).to_broadcast([P, HB, 4]),
+                    op=ALU.add,
+                )
+
         def stage1(u, h):
-            bank = ps_g.tile([P, 2, UT], F32, name="gb")
+            bank = ps_g.tile([P, 2, UT], F32, name="bank1")
             for i in range(2):
-                mx1(bank[:, i, :], 2 * h + i, u, 0, UT)
-            if u in A_UNITS:
-                if h == 0:
-                    st["ab", u] = work.tile([P, 2, E, 4, UB], F32, name="ab", bufs=3, align_bytes=64)
+                matmul1(bank[:, i, :], 2 * h + i, u, 0, UT)
+            made["bank1", u, h] = bank
+
+        def stage1_out(u, h):
+            bank = made["bank1", u, h]
+            if u in REDUCED:
+                if ("g1", u) not in made:
+                    made["g1", u] = work.tile([P, 2 * 4, UB, E], F32, name="g1", bufs=1)
+                nc.scalar.copy(
+                    out=made["g1", u][:, 2 * h : 2 * h + 2, :, :].rearrange("p f b e -> p (f b e)"),
+                    in_=bank[:].rearrange("p i n -> p (i n)"),
+                )
+            else:
+                if ("abs", u) not in made:
+                    made["abs", u] = work.tile([P, G, E, 4, UB], F32, name="abs", bufs=3, align_bytes=64)
                 nc.scalar.activation(
-                    out=st["ab", u][:, h // 2, :, 2 * (h % 2) : 2 * (h % 2) + 2, :],
+                    out=made["abs", u][:, h // 2, :, 2 * (h % 2) : 2 * (h % 2) + 2, :],
                     in_=bank[:].rearrange("p i (b e) -> p e i b", e=E),
                     func=ACT.Abs,
                 )
-            else:
-                if h == 0:
-                    st["g1", u] = work.tile([P, NF, UB, E], F32, name="g1", bufs=2)
-                nc.scalar.copy(
-                    out=st["g1", u][:, 2 * h : 2 * h + 2, :, :].rearrange("p f b e -> p (f b e)"),
-                    in_=bank[:].rearrange("p i n -> p (i n)"),
-                )
 
         def radius_sum(u, g):
-            if g == 0:
-                st["rt", u] = ps_x.tile([P, 2, P], F32, name="tt")
-            rt = st["rt", u]
-            for e in range(E):
-                nc.tensor.matmul(
-                    out=rt[:, g, :],
-                    lhsT=st["ab", u][:, g, e, :, :].rearrange("p t b -> p (t b)"),
-                    rhs=ident[:],
-                    is_transpose=True,
-                    start=(e == 0),
-                    stop=(e == E - 1),
-                )
-            if g == 1:
-                st["rts", u] = work.tile([P, 2, P], F32, name="rts", align_bytes=64)
-                nc.scalar.copy(out=st["rts", u][:], in_=rt[:])
+            if u in REDUCED:
+                if g == 0:
+                    rad = work.tile([P, 2 * 4, UB], F32, name="rad", bufs=1)
+                    nc.vector.tensor_reduce(
+                        out=rad[:].rearrange("p f b -> p (f b)"),
+                        in_=made["g1", u][:].rearrange("p f b e -> p (f b) e"),
+                        axis=AX.X,
+                        op=ALU.add,
+                        apply_absolute_value=True,
+                    )
+                    made["rad", u] = rad[:].rearrange("p (g t) b -> p g b t", g=G)
+            else:
+                if ("rad_t", u) not in made:
+                    made["rad_t", u] = ps_x.tile([P, G, P], F32, name="turned")
+                for e in range(E):
+                    nc.tensor.matmul(
+                        out=made["rad_t", u][:, g, :],
+                        lhsT=made["abs", u][:, g, e, :, :].rearrange("p t b -> p (t b)"),
+                        rhs=ident[:],
+                        is_transpose=True,
+                        start=(e == 0),
+                        stop=(e == E - 1),
+                    )
+
+        def radius_out(u):
+            if u not in REDUCED:
+                made["rad_s", u] = work.tile([P, G, P], F32, name="rad_s", align_bytes=64)
+                nc.scalar.copy(out=made["rad_s", u][:], in_=made["rad_t", u][:])
 
         def radius_back(u):
-            rb = ps_x.tile([P, 2, P], F32, name="tt")
-            for g in range(2):
-                nc.tensor.transpose(rb[:, g, :], st["rts", u][:, g, :], ident[:])
-            st["rad", u] = rb[:].rearrange("p g (t b) -> p g b t", t=4)
-
-        def radius_reduce(u):
-            rad = work.tile([P, NF, UB], F32, name="rad")
-            nc.vector.tensor_reduce(
-                out=rad[:].rearrange("p f b -> p (f b)"),
-                in_=st["g1", u][:].rearrange("p f b e -> p (f b) e"),
-                axis=AX.X,
-                op=ALU.add,
-                apply_absolute_value=True,
-            )
-            st["rad", u] = rad[:].rearrange("p (g t) b -> p g b t", g=2)
+            if u not in REDUCED:
+                bank = ps_x.tile([P, G, P], F32, name="turned")
+                for g in range(G):
+                    nc.tensor.transpose(bank[:, g, :], made["rad_s", u][:, g, :], ident[:])
+                made["rad", u] = bank[:].rearrange("p g (t b) -> p g b t", t=4)
 
         def inverse(u):
-            rs = work.tile([P, 2, UB, 4], F32, name="rs")
-            nc.scalar.activation(out=rs[:], in_=st["rad", u], func=ACT.Abs_reciprocal_sqrt, scale=2.0, bias=EPS)
-            inv = work.tile([P, 2, UB, 4], F32, name="inv")
+            rs = work.tile([P, G, UB, 4], F32, name="rs")
+            nc.scalar.activation(
+                out=rs[:], in_=made["rad", u], func=ACT.Abs_reciprocal_sqrt, scale=2.0, bias=EPS
+            )
+            inv = work.tile([P, G, UB, 4], F32, name="inv")
             nc.scalar.activation(out=inv[:], in_=rs[:], func=ACT.Square)
-            st["inv", u] = inv
+            made["inv", u] = inv
 
-        def part(n, u):
-            if (n, u // 2) not in st:
-                st[n, u // 2] = work.tile([P, 2, 2 * UB, 4], F32, name=n)
-            return st[n, u // 2][:, :, UB * (u % 2) : UB * (u % 2 + 1), :]
+        def of_unit(name, u):
+            if (name, u // 2) not in made:
+                made[name, u // 2] = work.tile([P, G, PAIR, 4], F32, name=name)
+            return made[name, u // 2][:, :, UB * (u % 2) : UB * (u % 2 + 1), :]
 
-        def centre(b0, nb):
-            return c1i[:, :, b0 : b0 + nb, :]
+        def slope_x(u):
+            x = work.tile([P, G, UB, 4], F32, name="x")
+            nc.vector.scalar_tensor_tensor(
+                out=x[:],
+                in0=c1[:, :, UB * u : UB * (u + 1), :],
+                scalar=0.5 * EPS,
+                in1=made["inv", u][:],
+                op0=ALU.subtract,
+                op1=ALU.mult,
+            )
+            made["slope_x", u] = x
 
-        def stage1_centre(h, g):
-            bank = ps_g.tile([P, 4, P], F32, name="gb")
-            for t in range(4):
-                mx1(bank[:, t, :], 4 * g + t, "c", P * h, P)
+        def slope_y(u):
+            nc.scalar.activation(out=of_unit("y", u), in_=made["slope_x", u][:], func=ACT.Relu, bias=0.5)
+
+        def slope_l(u):
             nc.vector.tensor_tensor(
-                out=c1i[:, g, P * h : P * (h + 1), :],
-                in0=bank[:].rearrange("p t b -> p b t"),
-                in1=b1f[:, g, :].unsqueeze(1).to_broadcast([P, P, 4]),
-                op=ALU.add,
+                out=of_unit("l", u), in0=c1[:, :, UB * u : UB * (u + 1), :], in1=made["rad", u], op=ALU.subtract
             )
 
-        def spread_k():
-            nc.vector.tensor_copy(out=b1f[:], in_=b1c[:])
-            nc.vector.tensor_copy(out=kful[:], in_=kc[:].unsqueeze(2).to_broadcast([P, 2, UB, 4]))
-
-        def slope(u):
-            x = work.tile([P, 2, UB, 4], F32, name="x")
-            nc.vector.scalar_tensor_tensor(out=x[:], in0=centre(UB * u, UB), scalar=0.5 * EPS, in1=st["inv", u][:], op0=ALU.subtract, op1=ALU.mult)
-            nc.scalar.activation(out=part("y", u), in_=x[:], func=ACT.Relu, bias=0.5)
-            nc.vector.tensor_tensor(out=part("l", u), in0=centre(UB * u, UB), in1=st["rad", u], op=ALU.subtract)
-
-        def slope2(u):
-            nc.vector.scalar_tensor_tensor(out=part("klam", u), in0=part("y", u), scalar=1.0, in1=kful[:], op0=ALU.min, op1=ALU.mult)
-
-        def centre_z(w):
-            z = work.tile([P, 2, 2 * UB, 4], F32, name="z")
-            nc.scalar.activation(out=z[:], in_=st["l", w][:], func=ACT.Relu, scale=-0.5)
-            st["z", w] = z
-
-        def centre_mu(w):
-            h, v = divmod(w, 2)
-            nc.vector.tensor_tensor(
-                out=mu_t[h][:, :, 2 * UB * v : 2 * UB * (v + 1)].rearrange("p (g t) b -> p g t b", g=2),
-                in0=st["z", w][:].rearrange("p g b t -> p g t b"),
-                in1=st["y", w][:].rearrange("p g b t -> p g t b"),
-                op=ALU.mult,
+        def slope_klam(u):
+            nc.vector.scalar_tensor_tensor(
+                out=of_unit("klam", u), in0=of_unit("y", u), scalar=1.0, in1=k_spread[:], op0=ALU.min, op1=ALU.mult
             )
 
-        def centre_hc(w):
-            s = work.tile([P, 2, 2 * UB, 4], F32, name="s")
-            nc.vector.tensor_tensor(out=s[:], in0=centre(2 * UB * w, 2 * UB), in1=st["z", w][:], op=ALU.add)
-            h, v = divmod(w, 2)
-            nc.vector.tensor_tensor(out=hc_t[h][:, :, 2 * UB * v : 2 * UB * (v + 1), :], in0=st["klam", w][:], in1=s[:], op=ALU.mult)
-
-        def again(u, g, m):
-            gr = ps_r.tile([P, 4, P], F32, name="gr")
-            for t in range(4):
-                mx1(gr[:, t, :], 4 * g + t, u, P * m, P)
-            st["gr", u, g, m] = gr
+        def stage1_again(u, g, m):
+            if u not in REDUCED:
+                bank = ps_r.tile([P, 4, P], F32, name="bank_again")
+                for t in range(4):
+                    matmul1(bank[:, t, :], 4 * g + t, u, P * m, P)
+                made["again", u, g, m] = bank
 
         def product(u, g, m):
-            if ("hb", u) not in st:
-                st["hb", u] = work.tile([P, 2, 2, P * 4], BF16, name="hb", align_bytes=64)
+            if ("hg", u) not in made:
+                made["hg", u] = work.tile([P, 2, G, P * 4], BF16, name="hg", align_bytes=64)
             nb = UB // 2
-            fs = slice(4 * g, 4 * g + 4)
-            bs = slice(nb * m, nb * (m + 1))
-            if u in A_UNITS:
-                src = st["gr", u, g, m][:].rearrange("p t (b e) -> p b e t", e=E)
+            samples = slice(nb * m, nb * (m + 1))
+            if u in REDUCED:
+                g1 = made["g1", u][:, 4 * g : 4 * g + 4, samples, :].rearrange("p t b e -> p b t e")
             else:
-                src = st["g1", u][:, fs, bs, :].rearrange("p t b e -> p b e t")
+                g1 = made["again", u, g, m][:].rearrange("p t (b e) -> p b t e", e=E)
             nc.vector.tensor_tensor(
-                out=st["hb", u][:, m, g, :].rearrange("p (b e t) -> p b e t", e=E, t=4),
-                in0=src,
-                in1=part("klam", u)[:, g, bs, :].unsqueeze(2).to_broadcast([P, nb, E, 4]),
+                out=made["hg", u][:, m, g, :].rearrange("p (b e t) -> p b t e", e=E, t=4),
+                in0=g1,
+                in1=of_unit("klam", u)[:, g, samples, :].unsqueeze(3).to_broadcast([P, nb, 4, E]),
                 op=ALU.mult,
             )
 
-        def quant_h(u, m, w):
-            if ("hq", u) not in st:
-                hq = work.tile([P, 2, 2, P], U32, name="hq", align_bytes=64)
-                hs = work.tile([P, 2, 2, P], U8, name="hs", align_bytes=64)
-                st["hq", u] = (hq, hs)
-            hq, hs = st["hq", u]
+        def quantise_rows(u, m, parts):
+            if ("hq", u) not in made:
+                hq = work.tile([P, 2, G, P], U32, name="hq", align_bytes=64)
+                hs = work.tile([P, 2, G, P], U8, name="hs", align_bytes=64)
+                made["hq", u] = (hq, hs)
+            hq, hs = made["hq", u]
             nc.vector.quantize_mx(
-                out=hq[:, m : m + w, :, :].rearrange("p m g n -> p (m g n)").bitcast(FP8X4),
-                scales=hs[:, m : m + w, :, :].rearrange("p m g n -> p (m g n)"),
-                in_=st["hb", u][:, m : m + w, :, :].rearrange("p m g n -> p (m g n)"),
+                out=hq[:, m : m + parts, :, :].rearrange("p m g n -> p (m g n)").bitcast(FP8X4),
+                scales=hs[:, m : m + parts, :, :].rearrange("p m g n -> p (m g n)"),
+                in_=made["hg", u][:, m : m + parts, :, :].rearrange("p m g n -> p (m g n)"),
             )
 
-        def stage2(codes, scales, dst, on_vector=False):
-            ob = ps_o.tile([P, O], F32, name="ob")
-            for g in range(2):
+        def quantise_h(u):
+            if u < NU - 1:
+                quantise_rows(u, 0, 2)
+
+        def quantise_h_part(u, m):
+            if u == NU - 1:
+                quantise_rows(u, m, 1)
+
+        def matmul2(codes, code_scales):
+            bank = ps_o.tile([P, O], F32, name="bank2")
+            for g in range(G):
                 nc.tensor.matmul_mx(
-                    out=ob[:],
+                    out=bank[:],
                     lhsT=codes[:, g, :].bitcast(FP8X4),
-                    lhsT_scale=scales[:, g, :],
+                    lhsT_scale=code_scales[:, g, :],
                     rhs=w2w[:, g, :].bitcast(FP8X4),
                     rhs_scale=w2s[:, g, :],
                     start=(g == 0),
-                    stop=(g == 1),
+                    stop=(g == G - 1),
                 )
+            return bank
+
+        def store(bank, dst):
             res = outs.tile([P, O], F32, name="res")
-            if on_vector:
-                nc.vector.tensor_copy(out=res[:], in_=ob[:])
-            else:
-                nc.scalar.copy(out=res[:], in_=ob[:])
+            nc.scalar.copy(out=res[:], in_=bank[:])
             nc.sync.dma_start(out=dst, in_=res[:])
 
-        g2 = out_0.rearrange("b e o -> (b e) o")
+        g2_rows = out_0.rearrange("b e o -> (b e) o")
 
-        def finish(u, m):
-            hq, hs = st["hq", u]
+        def stage2(u, m):
+            hq, hs = made["hq", u]
+            made["bank2", u, m] = matmul2(hq[:, m, :, :], hs[:, m, :, :])
+
+        def stage2_out(u, m):
             r0 = UT * u + P * m
-            stage2(hq[:, m, :, :], hs[:, m, :, :], g2[r0 : r0 + P, :], on_vector=((u, m) in EXV))
+            store(made["bank2", u, m], g2_rows[r0 : r0 + P, :])
 
-        def half_mu(h, g):
-            if g == 0:
-                st["ms", h] = outs.tile([P, 2, P, 4], F32, name="ms")
-            ms = st["ms", h]
-            om = ps_o.tile([P, 4, P], F32, name="ob")
-            for t in range(4):
-                nc.tensor.transpose(om[:, t, :], mu_t[h][:, 4 * g + t, :], ident[:])
-            nc.scalar.copy(out=ms[:, g, :, :], in_=om[:].rearrange("b t p -> b p t"))
-            if g == 1:
-                nc.sync.dma_start(out=out_2[P * h : P * (h + 1), :], in_=ms[:].rearrange("b g p t -> b (g p t)"))
+        def centre_z(u):
+            if u % 2 == 1:
+                z = work.tile([P, G, PAIR, 4], F32, name="z")
+                nc.scalar.activation(out=z[:], in_=made["l", u // 2][:], func=ACT.Relu, scale=-0.5)
+                made["z", u // 2] = z
 
-        def half_c2(h):
-            cq = work.tile([P, 2, P], U32, name="cq", align_bytes=64)
-            cs = work.tile([P, 2, P], U8, name="cs", align_bytes=64)
-            nc.vector.quantize_mx(
-                out=cq[:].rearrange("p g n -> p (g n)").bitcast(FP8X4),
-                scales=cs[:].rearrange("p g n -> p (g n)"),
-                in_=hc_t[h][:].rearrange("p g n t -> p (g n t)"),
-            )
-            st["cq", h] = (cq, cs)
+        def centre_mu(u):
+            if u % 2 == 1:
+                b0 = PAIR * (u // 2) % HB
+                nc.vector.tensor_tensor(
+                    out=mu[PAIR * (u // 2) // HB][:, :, b0 : b0 + PAIR].rearrange("p (g t) b -> p g t b", g=G),
+                    in0=made["z", u // 2][:].rearrange("p g b t -> p g t b"),
+                    in1=made["y", u // 2][:].rearrange("p g b t -> p g t b"),
+                    op=ALU.mult,
+                )
 
-        def half_c2_out(h):
-            stage2(st["cq", h][0], st["cq", h][1], out_1[P * h : P * (h + 1), :])
+        def centre_h(u):
+            if u % 2 == 1:
+                b0 = PAIR * (u // 2)
+                s = work.tile([P, G, PAIR, 4], F32, name="s")
+                nc.vector.tensor_tensor(
+                    out=s[:], in0=c1[:, :, b0 : b0 + PAIR, :], in1=made["z", u // 2][:], op=ALU.add
+                )
+                nc.vector.tensor_tensor(
+                    out=hc[b0 // HB][:, :, b0 % HB : b0 % HB + PAIR, :],
+                    in0=made["klam", u // 2][:],
+                    in1=s[:],
+                    op=ALU.mult,
+                )
 
-        def radius_start(u, g):
-            if u in A_UNITS:
-                radius_sum(u, g)
-            elif g == 0:
-                radius_reduce(u)
-                inverse(u)
+        def half_ends(u):
+            return u % (NU // 2) == NU // 2 - 1
 
-        def radius_end(u):
-            if u in A_UNITS:
-                radius_back(u)
-                inverse(u)
+        def centre_quantise(u):
+            if half_ends(u):
+                cq = work.tile([P, G, HB], U32, name="cq", align_bytes=64)
+                cs = work.tile([P, G, HB], U8, name="cs", align_bytes=64)
+                nc.vector.quantize_mx(
+                    out=cq[:].rearrange("p g n -> p (g n)").bitcast(FP8X4),
+                    scales=cs[:].rearrange("p g n -> p (g n)"),
+                    in_=hc[UB * u // HB][:].rearrange("p g n t -> p (g n t)"),
+                )
+                made["cq", u] = (cq, cs)
 
-        def recompute(u, g, m):
-            if u in A_UNITS:
-                again(u, g, m)
+        def centre_stage2(u):
+            if half_ends(u):
+                made["bank2_c", u] = matmul2(*made["cq", u])
+
+        def centre_stage2_out(u):
+            if half_ends(u):
+                b0 = UB * (u + 1) - HB
+                store(made["bank2_c", u], out_1[b0 : b0 + HB, :])
+
+        def mu_turn(u, g):
+            if half_ends(u):
+                bank = ps_o.tile([P, 4, P], F32, name="bank2")
+                for t in range(4):
+                    nc.tensor.transpose(bank[:, t, :], mu[UB * u // HB][:, 4 * g + t, :], ident[:])
+                made["mu_t", u, g] = bank
+
+        def mu_out(u, g):
+            if half_ends(u):
+                b0 = UB * (u + 1) - HB
+                m = outs.tile([P, P, 4], F32, name="mu_rows")
+                nc.scalar.copy(out=m[:], in_=made["mu_t", u, g][:].rearrange("b t p -> b p t"))
+                nc.sync.dma_start(
+                    out=out_2[b0 : b0 + HB, 512 * g : 512 * (g + 1)], in_=m[:].rearrange("b p t -> b (p t)")
+                )
+
+        calls = {
+            "permute_w1": permute_w1,
+            "spread_constants": spread_constants,
+            "widen": widen,
+            "turn": turn,
+            "turn_out": turn_out,
+            "quantise_x": quantise_x,
+            "centre_stage1": centre_stage1,
+            "centre_stage1_out": centre_stage1_out,
+            "stage1": stage1,
+            "stage1_out": stage1_out,
+            "radius_sum": radius_sum,
+            "radius_out": radius_out,
+            "radius_back": radius_back,
+            "inverse": inverse,
+            "slope_x": slope_x,
+            "slope_y": slope_y,
+            "slope_l": slope_l,
+            "slope_klam": slope_klam,
+            "stage1_again": stage1_again,
+            "product": product,
+            "quantise_h": quantise_h,
+            "quantise_h_part": quantise_h_part,
+            "stage2": stage2,
+            "stage2_out": stage2_out,
+            "centre_z": centre_z,
+            "centre_mu": centre_mu,
+            "centre_h": centre_h,
+            "centre_quantise": centre_quantise,
+            "centre_stage2": centre_stage2,
+            "centre_stage2_out": centre_stage2_out,
+            "mu_turn": mu_turn,
+            "mu_out": mu_out,
+        }
 
         ctx.enter_context(tc.manual_schedule())
-        widen(0)
-        widen(1)
-        permute_w1()
-        turn(0)
-        turn(1)
-        quant_x(1)
-        widen(2)
-        quant_x(0)
-        radius_end(0)
-        turn("c")
-        stage1(1, 0)
-        spread_k()
-        stage1(0, 0)
-        stage1(0, 2)
-        recompute(0, 1, 0)
-        radius_start(0, 1)
-        stage1(0, 3)
-        stage1(0, 1)
-        recompute(0, 0, 0)
-        stage1(1, 1)
-        stage1(1, 2)
-        quant_x("c")
-        stage1(1, 3)
-        widen(3)
-        turn(2)
-        radius_start(0, 0)
-        stage1_centre(0, 0)
-        stage1_centre(0, 1)
-        turn(3)
-        slope(0)
-        radius_start(1, 0)
-        radius_start(1, 1)
-        quant_x(2)
-        radius_end(1)
-        stage1(2, 0)
-        stage1(2, 1)
-        slope2(0)
-        stage1(2, 2)
-        widen(4)
-        for u in range(NU + 1):
-            if u < NU:
-                product(u, 0, 0)
-            if u < NU and u % 2 == 1:
-                centre_mu(u // 2)
-            if u > 0:
-                finish(u - 1, 0)
-            if u < NU:
-                product(u, 1, 0)
-            if u < NU and u % 2 == 1:
-                centre_hc(u // 2)
-            if u < NU:
-                recompute(u, 0, 1)
-            if u + 2 < NU:
-                stage1(u + 2, 3)
-            if u + 1 < NU:
-                slope(u + 1)
-            if u + 3 < NU:
-                quant_x(u + 3)
-            if u < NU:
-                recompute(u, 1, 1)
-            if u + 1 < NU and u % 2 == 0:
-                centre_z((u + 1) // 2)
-            if u < NU:
-                product(u, 0, 1)
-            if u == 1:
-                stage1_centre(1, 1)
-            if u % 4 == 3:
-                half_mu(u // 4, 0)
-            if u + 2 < NU:
-                radius_start(u + 2, 0)
-            if u % 4 == 3:
-                half_c2(u // 4)
-            if u > 0:
-                finish(u - 1, 1)
-            if u == NU - 1:
-                quant_h(u, 0, 1)
-            if u + 4 < NU:
-                turn(u + 4)
-            if u == 1:
-                stage1_centre(1, 0)
-            if u % 4 == 3:
-                half_mu(u // 4, 1)
-            if u + 1 < NU:
-                recompute(u + 1, 0, 0)
-            if u + 3 < NU:
-                stage1(u + 3, 0)
-            if u + 2 < NU:
-                radius_start(u + 2, 1)
-            if u + 3 < NU:
-                stage1(u + 3, 1)
-            if u < NU:
-                product(u, 1, 1)
-            if u == NU - 1:
-                quant_h(u, 1, 1)
-            if u + 1 < NU:
-                recompute(u + 1, 1, 0)
-            if u + 2 < NU:
-                radius_end(u + 2)
-            if u + 3 < NU:
-                stage1(u + 3, 2)
-            if u % 4 == 3:
-                half_c2_out(u // 4)
-            if u + 5 < NU:
-                widen(u + 5)
-            if u + 1 < NU:
-                slope2(u + 1)
-            if u < NU - 1:
-                quant_h(u, 0, 2)
+        for entry in PROLOGUE:
+            calls[entry[0]](*entry[1:])
+        for v in range(NU + 1):
+            for entry in LOOP:
+                u = v + entry[1]
+                if 0 <= u < NU:
+                    calls[entry[0]](u, *entry[2:])

@@ -28,33 +28,37 @@ FLOPS = 2 * (B + B * E) * (D * F + F * O)
 CENTRE = "c"
 REDUCED = (0,)
 
-VECTOR_PIECES = (8, 0, 8, 8, 6, 0, 0, 6)
+VECTOR_PIECES = (6, 8, 8, 8, 8, 2, 0, 6)
 
 PROLOGUE = (
-    ("widen", 1, 0), ("widen", 0, 0), ("widen", 1, 1), ("widen", 0, 1), ("permute_w1", 0), ("turn", 0),
-    ("turn_out", 0), ("turn", 1), ("quantise_x", 0), ("widen", 2, 0), ("turn_out", 1), ("widen", 2, 1),
-    ("turn", CENTRE), ("stage1", 0, 0), ("turn_out", CENTRE), ("stage1", 0, 1), ("stage1_out", 0, 0),
-    ("stage1", 0, 3), ("widen", 3, 0), ("quantise_x", 1), ("stage1_out", 0, 1), ("stage1", 1, 0),
-    ("stage1_out", 0, 3), ("stage1", 0, 2), ("stage1_out", 1, 0), ("stage1", 1, 1), ("stage1_out", 0, 2),
-    ("widen", 3, 1), ("quantise_x", CENTRE), ("stage1", 1, 2), ("stage1_out", 1, 1), ("stage1_out", 1, 2),
-    ("widen", 4, 0), ("spread_constants", 0), ("stage1", 1, 3), ("turn", 2), ("centre_stage1", 0, 0),
-    ("stage1_out", 1, 3), ("centre_stage1", 0, 1), ("turn_out", 2), ("widen", 4, 1), ("radius_sum", 1, 1),
-    ("turn", 3), ("radius_sum", 0, 0), ("centre_stage1_out", 0, 0), ("centre_stage1_out", 0, 1), ("inverse", 0),
-    ("quantise_x", 2), ("radius_sum", 1, 0), ("turn_out", 3), ("slope_x", 0), ("slope_y", 0), ("radius_out", 1),
-    ("stage1", 2, 0), ("stage1", 2, 1), ("stage1_out", 2, 0), ("stage1_out", 2, 1), ("radius_back", 1),
-    ("slope_l", 0), ("inverse", 1), ("slope_klam", 0),
+    ("load_tables", 0),
+    ("widen", 0, 0), ("widen", 0, 1), ("widen", 1, 0), ("turn", 0), ("widen", 1, 1), ("turn_out", 0), ("turn", 1),
+    ("permute_w1", 0), ("quantise_x", 0), ("widen", 2, 0), ("turn", CENTRE), ("stage1", 0, 1), ("turn_out", 1),
+    ("turn_out", CENTRE), ("quantise_x", 1), ("widen", 4, 0), ("stage1", 0, 0), ("stage1_out", 0, 1),
+    ("widen", 2, 1), ("stage1", 0, 3), ("stage1_out", 0, 0), ("stage1", 1, 0), ("spread_constants", 0),
+    ("stage1_out", 0, 3), ("widen", 3, 0), ("stage1", 0, 2), ("widen", 3, 1), ("stage1_out", 1, 0),
+    ("quantise_x", CENTRE), ("stage1", 1, 1), ("stage1_out", 0, 2), ("stage1_out", 1, 1), ("stage1", 1, 2),
+    ("stage1_out", 1, 2), ("stage1", 1, 3), ("radius_sum", 0, 0), ("turn", 2), ("stage1_out", 1, 3),
+    ("centre_stage1", 0, 0), ("centre_stage1", 0, 1), ("turn_out", 2), ("turn", 3), ("inverse", 0),
+    ("radius_sum", 1, 1), ("turn_out", 3), ("radius_sum", 1, 0), ("centre_stage1_out", 0, 0),
+    ("centre_stage1_out", 0, 1), ("quantise_x", 2), ("slope_x", 0), ("slope_y", 0), ("radius_out", 1),
+    ("slope_l", 0), ("widen", 4, 1), ("stage1", 2, 0), ("stage1_out", 2, 0), ("stage1", 2, 1), ("stage1_out", 2, 1),
+    ("slope_klam", 0),
 )
 LOOP = (
-    ("centre_mu", 0), ("product", 0, 0, 0), ("stage2", -1, 0), ("product", 0, 1, 0), ("mu_turn", 0, 0),
-    ("stage1", 2, 3), ("stage1_again", 0, 0, 1), ("stage1", 2, 2), ("stage2_out", -1, 0), ("stage1_again", 0, 1, 1),
-    ("radius_sum", 2, 0), ("quantise_x", 3), ("centre_h", 0), ("mu_out", 0, 0), ("slope_l", 1), ("slope_x", 1),
-    ("mu_turn", 0, 1), ("stage1_out", 2, 3), ("centre_stage1", 3, 0), ("stage2", -1, 1), ("stage1_out", 2, 2),
-    ("mu_out", 0, 1), ("centre_stage1", 3, 1), ("quantise_h_part", 0, 0), ("centre_quantise", 0), ("turn", 4),
-    ("product", 0, 0, 1), ("widen", 5, 0), ("centre_stage1_out", 3, 0), ("slope_y", 1), ("centre_stage1_out", 3, 1),
-    ("centre_z", 1), ("stage2_out", -1, 1), ("widen", 5, 1), ("radius_sum", 2, 1), ("stage1", 3, 0),
-    ("stage1_again", 1, 0, 0), ("turn_out", 4), ("radius_out", 2), ("stage1_out", 3, 0), ("stage1", 3, 1),
-    ("product", 0, 1, 1), ("stage1_again", 1, 1, 0), ("radius_back", 2), ("stage1_out", 3, 1), ("slope_klam", 1),
-    ("quantise_h_part", 0, 1), ("centre_stage2", 0), ("quantise_h", 0), ("inverse", 2), ("centre_stage2_out", 0),
+    ("quantise_x", 3), ("mu_turn", 2, 0, 0), ("radius_back", 1), ("centre_mu", 0), ("mu_out", 2, 0, 0),
+    ("stage2", -1, 0), ("inverse", 1), ("product", 0, 0, 0), ("mu_turn", 0, 1, 0), ("product", 0, 1, 0),
+    ("stage1", 2, 3), ("stage1_out", 2, 3), ("stage1_again", 0, 0, 1), ("slope_l", 1), ("centre_h", 0),
+    ("stage1", 2, 2), ("stage2_out", -1, 0), ("stage1_again", 0, 1, 1), ("quantise_h_part", 0, 0),
+    ("centre_quantise", 3, 0), ("stage1_out", 2, 2), ("widen", 5, 0), ("turn", 4), ("centre_quantise", 0, 1),
+    ("mu_turn", 2, 0, 1), ("slope_x", 1), ("mu_turn", 0, 1, 1), ("radius_sum", 2, 0), ("mu_out", 0, 1, 0),
+    ("centre_stage1", 3, 1), ("slope_y", 1), ("stage2", -1, 1), ("centre_stage1", 3, 0), ("turn_out", 4),
+    ("product", 0, 0, 1), ("mu_out", 0, 1, 1), ("product", 0, 1, 1), ("radius_sum", 2, 1), ("centre_z", 1),
+    ("mu_out", 2, 0, 1), ("centre_stage1_out", 3, 1), ("stage2_out", -1, 1), ("radius_out", 2),
+    ("centre_stage2", 0, 1), ("centre_stage1_out", 3, 0), ("stage1", 3, 0), ("centre_stage2", 1, 0), ("widen", 5, 1),
+    ("stage1_again", 1, 0, 0), ("slope_klam", 1), ("quantise_h", 0), ("stage1", 3, 1), ("stage1_again", 1, 1, 0),
+    ("stage1_out", 3, 0), ("centre_stage2_out", 0, 1), ("centre_stage2_out", 1, 0), ("stage1_out", 3, 1),
+    ("quantise_h_part", 0, 1),
 )
 
 
@@ -124,6 +128,9 @@ def tile_reluzonotopescaledgeneratormap_kernel(
         c1 = keep.tile([P, G, B, 4], F32, name="c1")
         mu = [keep.tile([P, 2 * 4, HB], F32, name="mu%d" % h) for h in range(2)]
         hc = [keep.tile([P, G, HB, 4], BF16, name="hc%d" % h, align_bytes=64) for h in range(2)]
+        one = keep.tile([P, 1], F32, name="one")
+        warm = keep.tile([P, 1], F32, name="warm")
+        nc.vector.memset(one[:], 1.0)
         made = {}
 
         def permute_w1(u):
@@ -135,6 +142,9 @@ def tile_reluzonotopescaledgeneratormap_kernel(
                 out=w1s[:].rearrange("p (g t m) -> p g t m", g=G, t=4),
                 in_=w1s_raw[:].rearrange("p (g m t) -> p g t m", g=G, t=4),
             )
+
+        def load_tables(u):
+            nc.scalar.activation(out=warm[:], in_=one[:], func=ACT.Abs_reciprocal_sqrt, scale=2.0, bias=EPS)
 
         def spread_constants(u):
             nc.vector.tensor_copy(out=b1_f32[:], in_=b1_raw[:])
@@ -410,47 +420,44 @@ def tile_reluzonotopescaledgeneratormap_kernel(
                     op=ALU.mult,
                 )
 
-        def half_ends(u):
-            return u % (NU // 2) == NU // 2 - 1
-
-        def centre_quantise(u):
-            if half_ends(u):
+        def centre_quantise(u, h):
+            if u == NU - 1:
                 cq = work.tile([P, G, HB], U32, name="cq", align_bytes=64)
                 cs = work.tile([P, G, HB], U8, name="cs", align_bytes=64)
                 nc.vector.quantize_mx(
                     out=cq[:].rearrange("p g n -> p (g n)").bitcast(FP8X4),
                     scales=cs[:].rearrange("p g n -> p (g n)"),
-                    in_=hc[UB * u // HB][:].rearrange("p g n t -> p (g n t)"),
+                    in_=hc[h][:].rearrange("p g n t -> p (g n t)"),
                 )
-                made["cq", u] = (cq, cs)
+                made["cq", h] = (cq, cs)
 
-        def centre_stage2(u):
-            if half_ends(u):
-                made["bank2_c", u] = matmul2(*made["cq", u])
+        def centre_stage2(u, h):
+            if u == NU - 1:
+                made["bank2_c", h] = matmul2(*made["cq", h])
 
-        def centre_stage2_out(u):
-            if half_ends(u):
-                b0 = UB * (u + 1) - HB
-                store(made["bank2_c", u], out_1[b0 : b0 + HB, :])
+        def centre_stage2_out(u, h):
+            if u == NU - 1:
+                store(made["bank2_c", h], out_1[HB * h : HB * (h + 1), :])
 
-        def mu_turn(u, g):
-            if half_ends(u):
+        def mu_turn(u, h, g):
+            if u == NU - 1:
                 bank = ps_o.tile([P, 4, P], F32, name="bank2")
                 for t in range(4):
-                    nc.tensor.transpose(bank[:, t, :], mu[UB * u // HB][:, 4 * g + t, :], ident[:])
-                made["mu_t", u, g] = bank
+                    nc.tensor.transpose(bank[:, t, :], mu[h][:, 4 * g + t, :], ident[:])
+                made["mu_t", h, g] = bank
 
-        def mu_out(u, g):
-            if half_ends(u):
-                b0 = UB * (u + 1) - HB
-                m = outs.tile([P, P, 4], F32, name="mu_rows")
-                nc.scalar.copy(out=m[:], in_=made["mu_t", u, g][:].rearrange("b t p -> b p t"))
+        def mu_out(u, h, g):
+            if u == NU - 1:
+                mu_rows = outs.tile([P, P, 4], F32, name="mu_rows")
+                nc.scalar.copy(out=mu_rows[:], in_=made["mu_t", h, g][:].rearrange("b t p -> b p t"))
                 nc.sync.dma_start(
-                    out=out_2[b0 : b0 + HB, 512 * g : 512 * (g + 1)], in_=m[:].rearrange("b p t -> b (p t)")
+                    out=out_2[HB * h : HB * (h + 1), 512 * g : 512 * (g + 1)],
+                    in_=mu_rows[:].rearrange("b p t -> b (p t)"),
                 )
 
         calls = {
             "permute_w1": permute_w1,
+            "load_tables": load_tables,
             "spread_constants": spread_constants,
             "widen": widen,
             "turn": turn,

from contextlib import ExitStack

import concourse.mybir as mybir
from concourse.masks import make_identity

F32 = mybir.dt.float32
BF16 = mybir.dt.bfloat16
I32 = mybir.dt.int32
U32 = mybir.dt.uint32
U8 = mybir.dt.uint8
FP8 = mybir.dt.float8_e4m3fn
FP8X4 = mybir.dt.float8_e4m3fn_x4
ALU = mybir.AluOpType
ACT = mybir.ActivationFunctionType
AX = mybir.AxisListType

B, E, D, F, O = 256, 8, 512, 1024, 512
P = 128
G = F // 512
UB = 32
UT = UB * E
NU = B // UB
HB = 128
PAIR = 2 * UB
EPS = 1e-6
FLOPS = 2 * (B + B * E) * (D * F + F * O)

CENTRE = "c"
REDUCED = (0,)

VECTOR_PIECES = (6, 8, 8, 8, 8, 2, 0, 6)

PROLOGUE = (
    ("load_tables", 0),
    ("widen", 0, 0), ("widen", 0, 1), ("widen", 1, 0), ("turn", 0), ("widen", 1, 1), ("turn_out", 0), ("turn", 1),
    ("permute_w1", 0), ("quantise_x", 0), ("widen", 2, 0), ("turn", CENTRE), ("stage1", 0, 1), ("turn_out", 1),
    ("turn_out", CENTRE), ("quantise_x", 1), ("widen", 4, 0), ("stage1", 0, 0), ("stage1_out", 0, 1),
    ("widen", 2, 1), ("stage1", 0, 3), ("stage1_out", 0, 0), ("stage1", 1, 0), ("spread_constants", 0),
    ("stage1_out", 0, 3), ("widen", 3, 0), ("stage1", 0, 2), ("widen", 3, 1), ("stage1_out", 1, 0),
    ("quantise_x", CENTRE), ("stage1", 1, 1), ("stage1_out", 0, 2), ("stage1_out", 1, 1), ("stage1", 1, 2),
    ("stage1_out", 1, 2), ("stage1", 1, 3), ("radius_sum", 0, 0), ("turn", 2), ("stage1_out", 1, 3),
    ("centre_stage1", 0, 0), ("centre_stage1", 0, 1), ("turn_out", 2), ("turn", 3), ("inverse", 0),
    ("radius_sum", 1, 1), ("turn_out", 3), ("radius_sum", 1, 0), ("centre_stage1_out", 0, 0),
    ("centre_stage1_out", 0, 1), ("quantise_x", 2), ("slope_x", 0), ("slope_y", 0), ("radius_out", 1),
    ("slope_l", 0), ("widen", 4, 1), ("stage1", 2, 0), ("stage1_out", 2, 0), ("stage1", 2, 1), ("stage1_out", 2, 1),
    ("slope_klam", 0),
)
LOOP = (
    ("quantise_x", 3), ("mu_turn", 2, 0, 0), ("radius_back", 1), ("centre_mu", 0), ("mu_out", 2, 0, 0),
    ("stage2", -1, 0), ("inverse", 1), ("product", 0, 0, 0), ("mu_turn", 0, 1, 0), ("product", 0, 1, 0),
    ("stage1", 2, 3), ("stage1_out", 2, 3), ("stage1_again", 0, 0, 1), ("slope_l", 1), ("centre_h", 0),
    ("stage1", 2, 2), ("stage2_out", -1, 0), ("stage1_again", 0, 1, 1), ("quantise_h_part", 0, 0),
    ("centre_quantise", 3, 0), ("stage1_out", 2, 2), ("widen", 5, 0), ("turn", 4), ("centre_quantise", 0, 1),
    ("mu_turn", 2, 0, 1), ("slope_x", 1), ("mu_turn", 0, 1, 1), ("radius_sum", 2, 0), ("mu_out", 0, 1, 0),
    ("centre_stage1", 3, 1), ("slope_y", 1), ("stage2", -1, 1), ("centre_stage1", 3, 0), ("turn_out", 4),
    ("product", 0, 0, 1), ("mu_out", 0, 1, 1), ("product", 0, 1, 1), ("radius_sum", 2, 1), ("centre_z", 1),
    ("mu_out", 2, 0, 1), ("centre_stage1_out", 3, 1), ("stage2_out", -1, 1), ("radius_out", 2),
    ("centre_stage2", 0, 1), ("centre_stage1_out", 3, 0), ("stage1", 3, 0), ("centre_stage2", 1, 0), ("widen", 5, 1),
    ("stage1_again", 1, 0, 0), ("slope_klam", 1), ("quantise_h", 0), ("stage1", 3, 1), ("stage1_again", 1, 1, 0),
    ("stage1_out", 3, 0), ("centre_stage2_out", 0, 1), ("centre_stage2_out", 1, 0), ("stage1_out", 3, 1),
    ("quantise_h_part", 0, 1),
)


def tile_reluzonotopescaledgeneratormap_kernel(
    tc, c, gens_bytes, gens_scale, w1_words, w1_scales, b1, k, w2_words, w2_scales, out_0, out_1, out_2
):
    nc = tc.nc
    with ExitStack() as ctx:
        keep = ctx.enter_context(tc.tile_pool(name="keep", bufs=1))
        work = ctx.enter_context(tc.tile_pool(name="work", bufs=4))
        outs = ctx.enter_context(tc.tile_pool(name="outs", bufs=4))
        ps_x = ctx.enter_context(tc.psum_pool(name="ps_x", bufs=2))
        ps_g = ctx.enter_context(tc.psum_pool(name="ps_g", bufs=2))
        ps_r = ctx.enter_context(tc.psum_pool(name="ps_r", bufs=2))
        ps_o = ctx.enter_context(tc.psum_pool(name="ps_o", bufs=2))

        rows = gens_bytes.rearrange("b e d -> (b e) d")
        raw = []

        def load(u):
            r = keep.tile([P, 2, D], U8, name="raw%d" % u, align_bytes=64)
            nc.sync.dma_start(out=r[:], in_=rows[UT * u : UT * (u + 1), :].rearrange("(p j) d -> p j d", j=2))
            raw.append(r)

        w1s_raw = keep.tile([P, F], U8, name="w1s_raw", align_bytes=64)
        w2s = keep.tile([P, G, O], U8, name="w2s", align_bytes=64)
        nc.vector.memset(w1s_raw[:].bitcast(I32), 0)
        nc.vector.memset(w2s[:].rearrange("p g n -> p (g n)").bitcast(I32), 0)

        gsc = keep.tile([P, NU, 8], F32, name="gsc")
        scales = gens_scale.rearrange("b e q -> (b e q)").rearrange("(u p x) -> p u x", p=P, x=8)
        nc.sync.dma_start(out=gsc[:, 0:1, :], in_=scales[:, 0:1, :])
        load(0)
        nc.sync.dma_start(out=gsc[:, 1:NU, :], in_=scales[:, 1:NU, :])
        load(1)
        w1_raw = keep.tile([P, F], I32, name="w1_raw", align_bytes=64)
        nc.sync.dma_start(out=w1_raw[:], in_=w1_words[0].rearrange("p n t -> p (n t)").bitcast(I32))
        for q in range(4):
            nc.scalar.dma_start(
                out=w1s_raw[32 * q : 32 * q + 4, :].bitcast(I32), in_=w1_scales[0, 4 * q : 4 * q + 4, :].bitcast(I32)
            )
        c_rows = keep.tile([P, 2, D], BF16, name="c_rows", align_bytes=64)
        nc.sync.dma_start(out=c_rows[:], in_=c.rearrange("(p j) d -> p j d", j=2))
        b1_raw = keep.tile([P, G, 4], BF16, name="b1_raw")
        nc.scalar.dma_start(out=b1_raw[:], in_=b1.rearrange("(g p t) -> p g t", g=G, t=4))
        k_raw = keep.tile([P, G, 4], BF16, name="k_raw")
        nc.scalar.dma_start(out=k_raw[:], in_=k.rearrange("(g p t) -> p g t", g=G, t=4))
        for u in range(2, 4):
            load(u)
        w2w = keep.tile([P, G, O], I32, name="w2w", align_bytes=64)
        nc.sync.dma_start(out=w2w[:], in_=w2_words.rearrange("g p n t -> p g (n t)").bitcast(I32))
        for q in range(4):
            nc.sync.dma_start(
                out=w2s[32 * q : 32 * q + 4, :, :].bitcast(I32),
                in_=w2_scales[:, 4 * q : 4 * q + 4, :].rearrange("g r n -> r g n").bitcast(I32),
            )
        for u in range(4, NU):
            load(u)

        ident = keep.tile([P, P], F32, name="ident")
        make_identity(nc, ident[:])

        w1w = keep.tile([P, F], I32, name="w1w", align_bytes=64)
        w1s = keep.tile([P, F], U8, name="w1s", align_bytes=64)
        b1_f32 = keep.tile([P, G, 4], F32, name="b1_f32")
        k_spread = keep.tile([P, G, UB, 4], F32, name="k_spread")
        c1 = keep.tile([P, G, B, 4], F32, name="c1")
        mu = [keep.tile([P, 2 * 4, HB], F32, name="mu%d" % h) for h in range(2)]
        hc = [keep.tile([P, G, HB, 4], BF16, name="hc%d" % h, align_bytes=64) for h in range(2)]
        one = keep.tile([P, 1], F32, name="one")
        warm = keep.tile([P, 1], F32, name="warm")
        nc.vector.memset(one[:], 1.0)
        made = {}

        def permute_w1(u):
            nc.vector.tensor_copy(
                out=w1w[:].rearrange("p (g t m) -> p g t m", g=G, t=4),
                in_=w1_raw[:].rearrange("p (g m t) -> p g t m", g=G, t=4),
            )
            nc.vector.tensor_copy(
                out=w1s[:].rearrange("p (g t m) -> p g t m", g=G, t=4),
                in_=w1s_raw[:].rearrange("p (g m t) -> p g t m", g=G, t=4),
            )

        def load_tables(u):
            nc.scalar.activation(out=warm[:], in_=one[:], func=ACT.Abs_reciprocal_sqrt, scale=2.0, bias=EPS)

        def spread_constants(u):
            nc.vector.tensor_copy(out=b1_f32[:], in_=b1_raw[:])
            nc.vector.tensor_copy(out=k_spread[:], in_=k_raw[:].unsqueeze(2).to_broadcast([P, G, UB, 4]))

        def widen(u, j):
            if j == 0:
                made["x", u] = keep.tile([P, 2, D], BF16, name="x_rows", bufs=4, align_bytes=64)
            for q in range(4):
                i = 4 * j + q
                src = raw[u][:, j, P * q : P * (q + 1)].bitcast(FP8)
                dst = made["x", u][:, j, P * q : P * (q + 1)]
                if 4 * (q % 2) + 2 * j + q // 2 < VECTOR_PIECES[u]:
                    nc.vector.tensor_scalar(
                        out=dst, in0=src, scalar1=gsc[:, u, i : i + 1], scalar2=None, op0=ALU.mult
                    )
                else:
                    nc.scalar.activation(out=dst, in_=src, func=ACT.Copy, scale=gsc[:, u, i : i + 1])

        def turn(u):
            x_rows = c_rows if u == CENTRE else made["x", u]
            words = x_rows[:].rearrange("p j d -> p (j d)").bitcast(F32)
            bank = ps_x.tile([P, 4, P], F32, name="turned")
            for j in range(2):
                for w in range(2):
                    nc.tensor.transpose(bank[:, 2 * j + w, :], words[:, 256 * j + w : 256 * (j + 1) : 2], ident[:])
            made["turned", u] = bank

        def turn_out(u):
            xk = keep.tile([P, UT, 4], BF16, name="xk", bufs=4, align_bytes=64)
            nc.scalar.copy(
                out=xk[:].rearrange("p n t -> p (n t)").bitcast(F32).rearrange("p (r a) -> p r a", a=4),
                in_=made["turned", u][:].rearrange("p a r -> p r a"),
            )
            made["xk", u] = xk

        def quantise_x(u):
            xq = keep.tile([P, UT], U32, name="xq%s" % u, align_bytes=64)
            xs = keep.tile([P, UT], U8, name="xs%s" % u, align_bytes=64)
            nc.vector.quantize_mx(
                out=xq[:].bitcast(FP8X4), scales=xs[:], in_=made["xk", u][:].rearrange("p n t -> p (n t)")
            )
            made["xq", u] = (xq, xs)

        def matmul1(out, f, u, n0, n):
            xq, xs = made["xq", u]
            cols = slice(P * f, P * (f + 1))
            nc.tensor.matmul_mx(
                out=out,
                lhsT=w1w[:, cols].bitcast(FP8X4),
                lhsT_scale=w1s[:, cols],
                rhs=xq[:, n0 : n0 + n].bitcast(FP8X4),
                rhs_scale=xs[:, n0 : n0 + n],
                start=True,
                stop=True,
            )

        def centre_stage1(u, g):
            if u % (NU // 2) == 0:
                bank = ps_g.tile([P, 4, P], F32, name="bank1")
                for t in range(4):
                    matmul1(bank[:, t, :], 4 * g + t, CENTRE, UB * u, HB)
                made["bank_c", u, g] = bank

        def centre_stage1_out(u, g):
            if u % (NU // 2) == 0:
                nc.vector.tensor_tensor(
                    out=c1[:, g, UB * u : UB * u + HB, :],
                    in0=made["bank_c", u, g][:].rearrange("p t b -> p b t"),
                    in1=b1_f32[:, g, :].unsqueeze(1).to_broadcast([P, HB, 4]),
                    op=ALU.add,
                )

        def stage1(u, h):
            bank = ps_g.tile([P, 2, UT], F32, name="bank1")
            for i in range(2):
                matmul1(bank[:, i, :], 2 * h + i, u, 0, UT)
            made["bank1", u, h] = bank

        def stage1_out(u, h):
            bank = made["bank1", u, h]
            if u in REDUCED:
                if ("g1", u) not in made:
                    made["g1", u] = work.tile([P, 2 * 4, UB, E], F32, name="g1", bufs=1)
                nc.scalar.copy(
                    out=made["g1", u][:, 2 * h : 2 * h + 2, :, :].rearrange("p f b e -> p (f b e)"),
                    in_=bank[:].rearrange("p i n -> p (i n)"),
                )
            else:
                if ("abs", u) not in made:
                    made["abs", u] = work.tile([P, G, E, 4, UB], F32, name="abs", bufs=3, align_bytes=64)
                nc.scalar.activation(
                    out=made["abs", u][:, h // 2, :, 2 * (h % 2) : 2 * (h % 2) + 2, :],
                    in_=bank[:].rearrange("p i (b e) -> p e i b", e=E),
                    func=ACT.Abs,
                )

        def radius_sum(u, g):
            if u in REDUCED:
                if g == 0:
                    rad = work.tile([P, 2 * 4, UB], F32, name="rad", bufs=1)
                    nc.vector.tensor_reduce(
                        out=rad[:].rearrange("p f b -> p (f b)"),
                        in_=made["g1", u][:].rearrange("p f b e -> p (f b) e"),
                        axis=AX.X,
                        op=ALU.add,
                        apply_absolute_value=True,
                    )
                    made["rad", u] = rad[:].rearrange("p (g t) b -> p g b t", g=G)
            else:
                if ("rad_t", u) not in made:
                    made["rad_t", u] = ps_x.tile([P, G, P], F32, name="turned")
                for e in range(E):
                    nc.tensor.matmul(
                        out=made["rad_t", u][:, g, :],
                        lhsT=made["abs", u][:, g, e, :, :].rearrange("p t b -> p (t b)"),
                        rhs=ident[:],
                        is_transpose=True,
                        start=(e == 0),
                        stop=(e == E - 1),
                    )

        def radius_out(u):
            if u not in REDUCED:
                made["rad_s", u] = work.tile([P, G, P], F32, name="rad_s", align_bytes=64)
                nc.scalar.copy(out=made["rad_s", u][:], in_=made["rad_t", u][:])

        def radius_back(u):
            if u not in REDUCED:
                bank = ps_x.tile([P, G, P], F32, name="turned")
                for g in range(G):
                    nc.tensor.transpose(bank[:, g, :], made["rad_s", u][:, g, :], ident[:])
                made["rad", u] = bank[:].rearrange("p g (t b) -> p g b t", t=4)

        def inverse(u):
            rs = work.tile([P, G, UB, 4], F32, name="rs")
            nc.scalar.activation(
                out=rs[:], in_=made["rad", u], func=ACT.Abs_reciprocal_sqrt, scale=2.0, bias=EPS
            )
            inv = work.tile([P, G, UB, 4], F32, name="inv")
            nc.scalar.activation(out=inv[:], in_=rs[:], func=ACT.Square)
            made["inv", u] = inv

        def of_unit(name, u):
            if (name, u // 2) not in made:
                made[name, u // 2] = work.tile([P, G, PAIR, 4], F32, name=name)
            return made[name, u // 2][:, :, UB * (u % 2) : UB * (u % 2 + 1), :]

        def slope_x(u):
            x = work.tile([P, G, UB, 4], F32, name="x")
            nc.vector.scalar_tensor_tensor(
                out=x[:],
                in0=c1[:, :, UB * u : UB * (u + 1), :],
                scalar=0.5 * EPS,
                in1=made["inv", u][:],
                op0=ALU.subtract,
                op1=ALU.mult,
            )
            made["slope_x", u] = x

        def slope_y(u):
            nc.scalar.activation(out=of_unit("y", u), in_=made["slope_x", u][:], func=ACT.Relu, bias=0.5)

        def slope_l(u):
            nc.vector.tensor_tensor(
                out=of_unit("l", u), in0=c1[:, :, UB * u : UB * (u + 1), :], in1=made["rad", u], op=ALU.subtract
            )

        def slope_klam(u):
            nc.vector.scalar_tensor_tensor(
                out=of_unit("klam", u), in0=of_unit("y", u), scalar=1.0, in1=k_spread[:], op0=ALU.min, op1=ALU.mult
            )

        def stage1_again(u, g, m):
            if u not in REDUCED:
                bank = ps_r.tile([P, 4, P], F32, name="bank_again")
                for t in range(4):
                    matmul1(bank[:, t, :], 4 * g + t, u, P * m, P)
                made["again", u, g, m] = bank

        def product(u, g, m):
            if ("hg", u) not in made:
                made["hg", u] = work.tile([P, 2, G, P * 4], BF16, name="hg", align_bytes=64)
            nb = UB // 2
            samples = slice(nb * m, nb * (m + 1))
            if u in REDUCED:
                g1 = made["g1", u][:, 4 * g : 4 * g + 4, samples, :].rearrange("p t b e -> p b t e")
            else:
                g1 = made["again", u, g, m][:].rearrange("p t (b e) -> p b t e", e=E)
            nc.vector.tensor_tensor(
                out=made["hg", u][:, m, g, :].rearrange("p (b e t) -> p b t e", e=E, t=4),
                in0=g1,
                in1=of_unit("klam", u)[:, g, samples, :].unsqueeze(3).to_broadcast([P, nb, 4, E]),
                op=ALU.mult,
            )

        def quantise_rows(u, m, parts):
            if ("hq", u) not in made:
                hq = work.tile([P, 2, G, P], U32, name="hq", align_bytes=64)
                hs = work.tile([P, 2, G, P], U8, name="hs", align_bytes=64)
                made["hq", u] = (hq, hs)
            hq, hs = made["hq", u]
            nc.vector.quantize_mx(
                out=hq[:, m : m + parts, :, :].rearrange("p m g n -> p (m g n)").bitcast(FP8X4),
                scales=hs[:, m : m + parts, :, :].rearrange("p m g n -> p (m g n)"),
                in_=made["hg", u][:, m : m + parts, :, :].rearrange("p m g n -> p (m g n)"),
            )

        def quantise_h(u):
            if u < NU - 1:
                quantise_rows(u, 0, 2)

        def quantise_h_part(u, m):
            if u == NU - 1:
                quantise_rows(u, m, 1)

        def matmul2(codes, code_scales):
            bank = ps_o.tile([P, O], F32, name="bank2")
            for g in range(G):
                nc.tensor.matmul_mx(
                    out=bank[:],
                    lhsT=codes[:, g, :].bitcast(FP8X4),
                    lhsT_scale=code_scales[:, g, :],
                    rhs=w2w[:, g, :].bitcast(FP8X4),
                    rhs_scale=w2s[:, g, :],
                    start=(g == 0),
                    stop=(g == G - 1),
                )
            return bank

        def store(bank, dst):
            res = outs.tile([P, O], F32, name="res")
            nc.scalar.copy(out=res[:], in_=bank[:])
            nc.sync.dma_start(out=dst, in_=res[:])

        g2_rows = out_0.rearrange("b e o -> (b e) o")

        def stage2(u, m):
            hq, hs = made["hq", u]
            made["bank2", u, m] = matmul2(hq[:, m, :, :], hs[:, m, :, :])

        def stage2_out(u, m):
            r0 = UT * u + P * m
            store(made["bank2", u, m], g2_rows[r0 : r0 + P, :])

        def centre_z(u):
            if u % 2 == 1:
                z = work.tile([P, G, PAIR, 4], F32, name="z")
                nc.scalar.activation(out=z[:], in_=made["l", u // 2][:], func=ACT.Relu, scale=-0.5)
                made["z", u // 2] = z

        def centre_mu(u):
            if u % 2 == 1:
                b0 = PAIR * (u // 2) % HB
                nc.vector.tensor_tensor(
                    out=mu[PAIR * (u // 2) // HB][:, :, b0 : b0 + PAIR].rearrange("p (g t) b -> p g t b", g=G),
                    in0=made["z", u // 2][:].rearrange("p g b t -> p g t b"),
                    in1=made["y", u // 2][:].rearrange("p g b t -> p g t b"),
                    op=ALU.mult,
                )

        def centre_h(u):
            if u % 2 == 1:
                b0 = PAIR * (u // 2)
                s = work.tile([P, G, PAIR, 4], F32, name="s")
                nc.vector.tensor_tensor(
                    out=s[:], in0=c1[:, :, b0 : b0 + PAIR, :], in1=made["z", u // 2][:], op=ALU.add
                )
                nc.vector.tensor_tensor(
                    out=hc[b0 // HB][:, :, b0 % HB : b0 % HB + PAIR, :],
                    in0=made["klam", u // 2][:],
                    in1=s[:],
                    op=ALU.mult,
                )

        def centre_quantise(u, h):
            if u == NU - 1:
                cq = work.tile([P, G, HB], U32, name="cq", align_bytes=64)
                cs = work.tile([P, G, HB], U8, name="cs", align_bytes=64)
                nc.vector.quantize_mx(
                    out=cq[:].rearrange("p g n -> p (g n)").bitcast(FP8X4),
                    scales=cs[:].rearrange("p g n -> p (g n)"),
                    in_=hc[h][:].rearrange("p g n t -> p (g n t)"),
                )
                made["cq", h] = (cq, cs)

        def centre_stage2(u, h):
            if u == NU - 1:
                made["bank2_c", h] = matmul2(*made["cq", h])

        def centre_stage2_out(u, h):
            if u == NU - 1:
                store(made["bank2_c", h], out_1[HB * h : HB * (h + 1), :])

        def mu_turn(u, h, g):
            if u == NU - 1:
                bank = ps_o.tile([P, 4, P], F32, name="bank2")
                for t in range(4):
                    nc.tensor.transpose(bank[:, t, :], mu[h][:, 4 * g + t, :], ident[:])
                made["mu_t", h, g] = bank

        def mu_out(u, h, g):
            if u == NU - 1:
                mu_rows = outs.tile([P, P, 4], F32, name="mu_rows")
                nc.scalar.copy(out=mu_rows[:], in_=made["mu_t", h, g][:].rearrange("b t p -> b p t"))
                nc.sync.dma_start(
                    out=out_2[HB * h : HB * (h + 1), 512 * g : 512 * (g + 1)],
                    in_=mu_rows[:].rearrange("b p t -> b (p t)"),
                )

        calls = {
            "permute_w1": permute_w1,
            "load_tables": load_tables,
            "spread_constants": spread_constants,
            "widen": widen,
            "turn": turn,
            "turn_out": turn_out,
            "quantise_x": quantise_x,
            "centre_stage1": centre_stage1,
            "centre_stage1_out": centre_stage1_out,
            "stage1": stage1,
            "stage1_out": stage1_out,
            "radius_sum": radius_sum,
            "radius_out": radius_out,
            "radius_back": radius_back,
            "inverse": inverse,
            "slope_x": slope_x,
            "slope_y": slope_y,
            "slope_l": slope_l,
            "slope_klam": slope_klam,
            "stage1_again": stage1_again,
            "product": product,
            "quantise_h": quantise_h,
            "quantise_h_part": quantise_h_part,
            "stage2": stage2,
            "stage2_out": stage2_out,
            "centre_z": centre_z,
            "centre_mu": centre_mu,
            "centre_h": centre_h,
            "centre_quantise": centre_quantise,
            "centre_stage2": centre_stage2,
            "centre_stage2_out": centre_stage2_out,
            "mu_turn": mu_turn,
            "mu_out": mu_out,
        }

        ctx.enter_context(tc.manual_schedule())
        for entry in PROLOGUE:
            calls[entry[0]](*entry[1:])
        for v in range(NU + 1):
            for entry in LOOP:
                u = v + entry[1]
                if 0 <= u < NU:
                    calls[entry[0]](u, *entry[2:])
